import numpy as np
import ml_dtypes


def mxq(x, axis, fmt="e4m3"):
    dtype, down = {"e4m3": (ml_dtypes.float8_e4m3fn, 7), "e5m2": (ml_dtypes.float8_e5m2, 14)}[fmt]
    v = np.moveaxis(np.asarray(x, np.float32).astype(ml_dtypes.bfloat16).astype(np.float64), axis, -1)
    blocks = v.reshape(v.shape[:-1] + (-1, 32))
    amax = np.abs(blocks).max(-1, keepdims=True)
    byte = np.maximum(np.where(amax > 0, np.frexp(amax)[1] - 1 + 127, 0) - down, 1)
    scale = np.exp2(byte - 127.0)
    codes = (blocks / scale).astype(np.float32).astype(dtype).astype(np.float64)
    return np.moveaxis((codes * scale).reshape(v.shape), -1, axis)


WIDE = False


def mx_kscale(k):
    if not WIDE:
        return np.ones(k)
    levels = np.array([10, -10, 5, -5, 0])
    if k % 512:
        return np.exp2(np.random.permutation(np.resize(levels, k // 32))).repeat(32)
    a = np.empty((k // 512, 16))
    for p in range(k // 512):
        a[p, :8] = np.random.permutation(np.resize(levels, 8))
        for g in range(8):
            far = levels[np.abs(levels - a[p, g]) >= 10]
            a[p, g + 8] = far[np.random.randint(len(far))]
    return np.exp2(a.ravel()).repeat(32)


BF16 = ml_dtypes.bfloat16


def bf(x):
    return np.asarray(x, np.float32).astype(BF16)


def f64(x):
    return np.asarray(x).astype(np.float64)


E2M1 = np.array([0.0, 0.5, 1.0, 1.5, 2.0, 3.0, 4.0, 6.0, -0.0, -0.5, -1.0, -1.5, -2.0, -3.0, -4.0, -6.0])


def pack_weight(w, fmt):
    k, n = w.shape
    w = f64(bf(w)).reshape(k // 32, 32, n)
    amax = np.abs(w).max(1)
    if fmt == "e4m3":
        byte = np.frexp(amax)[1] - 1 + 127 - 7
    else:
        mant, ex = np.frexp(amax / 6.0)
        byte = np.where(mant > 0.5, ex, ex - 1) + 127
    byte = np.clip(np.where(amax > 0, byte, 1), 1, 254)
    scaled = (w * np.exp2(127.0 - byte)[:, None, :]).reshape(k, n).astype(np.float32)
    by_word = np.ascontiguousarray(scaled.reshape(k // 512, 128, 4, n).transpose(0, 1, 3, 2))
    if fmt == "e4m3":
        words = by_word.astype(ml_dtypes.float8_e4m3fn).view(np.uint8)
    else:
        c = by_word.astype(ml_dtypes.float4_e2m1fn).view(np.uint8) & 0xF
        words = c[..., 0::2] | (c[..., 1::2] << 4)
    return np.ascontiguousarray(words), np.ascontiguousarray(byte.astype(np.uint8).reshape(k // 512, 16, n))


def unpack_weight(words, scales, fmt):
    g, p, n, _ = words.shape
    if fmt == "e4m3":
        vals = np.ascontiguousarray(words).view(ml_dtypes.float8_e4m3fn).astype(np.float64)
    else:
        nib = np.empty((g, p, n, 4), np.uint8)
        nib[..., 0::2] = words & 0xF
        nib[..., 1::2] = words >> 4
        vals = E2M1[nib]
    vals = vals * np.repeat(np.exp2(scales.astype(np.float64) - 127.0), 8, axis=1)[..., None]
    return vals.transpose(0, 1, 3, 2).reshape(g * 512, n)
def pack4(w):
    words, scales = pack_weight(w, "e2m1")
    return words.reshape(words.shape[0], 128, -1), scales


def unpack4(words, scales):
    return unpack_weight(words.reshape(words.shape[0], 128, -1, 2), scales, "e2m1")


M, T, S, K, N, R, L = 2048, 8, 256, 1536, 1024, 512, 256


def draw0():
    s = mx_kscale(K)
    c = mx_kscale(N)
    u = mx_kscale(M)
    proj = np.random.standard_normal((N, R)) / np.sqrt(N) / c[:, None]
    proj_words, proj_scales = pack4(proj)
    return {"x": bf(np.random.standard_normal((M, K)) * s),
            "w": bf(np.random.standard_normal((K, N)) / np.sqrt(K) / s[:, None] * c),
            "time_pos": bf(0.5 * np.random.standard_normal((T, N)) * c),
            "space_pos": bf(0.5 * np.random.standard_normal((S, N)) * c),
            "gain": bf((1 + 0.1 * np.random.standard_normal(M)) * u),
            "proj_words": proj_words,
            "proj_scales": proj_scales,
            "pool": bf(np.random.standard_normal((L, M)) / np.sqrt(M) / u)}


def core(x, w, time_pos, space_pos, gain, proj_words, proj_scales, pool):
    e = mxq(f64(x), 1, "e4m3") @ mxq(f64(w), 0, "e4m3")
    z = e.reshape(T, S, N) + f64(time_pos)[:, None, :] + f64(space_pos)[None, :, :]
    h = z.reshape(M, N) * f64(gain)[:, None]
    feats = mxq(h, 1, "e4m3") @ unpack4(proj_words, proj_scales)
    latents = mxq(f64(pool), 1, "e4m3") @ mxq(h, 0, "e4m3")
    return feats, latents


def e4m3fn_bytes(y):
    return np.clip(np.asarray(y, np.float64), -448.0, 448.0).astype(np.float32).astype(ml_dtypes.float8_e4m3fn).view(np.uint8)


def e4m3fn_values(b):
    return np.asarray(b, np.uint8).view(ml_dtypes.float8_e4m3fn).astype(np.float64)


def setup_inputs():
    d = draw0()
    x0 = np.asarray(d['x']).astype(np.float64)
    s = (np.max(np.abs(x0), axis=(0,), keepdims=True) / 448.0).astype(np.float32)
    out = {}
    for k, v in d.items():
        if k == 'x':
            out['x_bytes'] = e4m3fn_bytes(x0 / s.astype(np.float64))
            out['x_scale'] = s
        else:
            out[k] = v
    return out


def reference(x_bytes, x_scale, w, time_pos, space_pos, gain, proj_words, proj_scales, pool):
    return core(e4m3fn_values(x_bytes) * x_scale.astype(np.float64), w, time_pos, space_pos, gain, proj_words, proj_scales, pool)

@@ -1,0 +1,389 @@
+from contextlib import ExitStack
+
+import concourse.mybir as mybir
+from concourse.masks import make_identity
+
+M, T, S, K, N, R, L = 2048, 8, 256, 1536, 1024, 512, 256
+FLOPS = 2 * (M * K * N + M * N * R + L * M * N)
+
+F32 = mybir.dt.float32
+BF16 = mybir.dt.bfloat16
+I32 = mybir.dt.int32
+U32 = mybir.dt.uint32
+U8 = mybir.dt.uint8
+F8 = mybir.dt.float8_e4m3fn
+F8X4 = mybir.dt.float8_e4m3fn_x4
+F4X4 = mybir.dt.float4_e2m1fn_x4
+COPY = mybir.ActivationFunctionType.Copy
+ADD = mybir.AluOpType.add
+MULT = mybir.AluOpType.mult
+
+P = 128
+KP = K // 512
+TILES = M // P
+HALF = 512
+CH = 256
+
+AT = {"widen":-1.8674,"turn_x":-1.6039,"quantize_x":-0.6549,"place0":-1.3658,"place1":-0.736,"embed0":-0.4106,"embed1":0.1152,"finish0":0.3843,"finish1":0.4498,"turn_h":1.1697,"quantize_hx":1.5792,"feats":2.2412,"group_h":5.151,"group_step":0.9683,"quantize_h":6.0619,"last_group":3.4646,"last_step":1.013,"last_quantize":5.1494,"pool0":3.3997,"pool_step":2.0081,"pool_q":0.9988,"wi00":-4.1691,"wi10":-2.4974,"wi20":-3.889,"wq00":-2.7189,"wq10":-1.6576,"wq20":-1.2366,"wi01":-0.8594,"wi11":-1.6815,"wi21":-0.9131,"wq01":0.0682,"wq11":0.0603,"wq21":-0.6822,"latents":17.205,"gain":-1.858,"place_rate":0.9955}
+DQ = {"x0a":-0.5647,"w00":-4.2437,"w10":-3.1927,"x0b":0.4036,"w20":-3.3619,"gain":-5.1961,"pos":2.7926,"w01":8.9419,"w11":0.6852,"w21":2.3029,"x":7.2407,"proj":22.0402,"pool":11.5476}
+ON_S = {"wi00":0,"wi10":1,"wi20":0,"wi01":1,"wi11":1,"wi21":0}
+H_ON_S = [0,0,1,0,1,0,1,1,0,0,1,1,0,0,0,0]
+
+
+def tile_tubelet_embed_pool_s8_kernel(
+    tc, x_bytes, x_scale, w, time_pos, space_pos, gain, proj_words, proj_scales, pool, out_0, out_1
+):
+    nc = tc.nc
+    with ExitStack() as ctx:
+        keep = ctx.enter_context(tc.tile_pool(name="keep", bufs=1))
+        work = ctx.enter_context(tc.tile_pool(name="work", bufs=2))
+        psum = ctx.enter_context(tc.psum_pool(name="psum", bufs=1))
+        ctx.enter_context(tc.manual_schedule())
+
+        scale_bc = keep.tile([P, K], F32, align_bytes=64)
+        nc.scalar.dma_start(out=scale_bc[:], in_=x_scale.rearrange("o k -> (o k)").partition_broadcast(P))
+        gain_bf = keep.tile([P, 4, 4], BF16)
+
+        ident = keep.tile([P, P], F32, align_bytes=64)
+        make_identity(nc, ident[:])
+        pos = keep.tile([P, 4, N], BF16, align_bytes=64)
+        nc.gpsimd.memset(pos[64:128].rearrange("p t d -> p (t d)").bitcast(F32), 0.0)
+        proj_s = keep.tile([P, 2, R], U8, align_bytes=64)
+        nc.gpsimd.memset(proj_s[:].rearrange("p g n -> p (g n)").bitcast(I32), 0)
+
+        x_rows = x_bytes.rearrange("(g p t) k -> g p t k", p=P, t=4)
+        xr = []
+        for s in range(TILES // 2):
+            xr.append(keep.tile([P, 2, K], U8, name="xr%d" % s, align_bytes=64))
+
+        def load_x(s, js):
+            g, t0 = s // 2, 2 * (s % 2)
+            nc.sync.dma_start(out=xr[s][:, js, :], in_=x_rows[g][:, t0 + js.start : t0 + js.stop, :])
+
+        w_rows = w.rearrange("(c p j) n -> c p j n", p=P, j=4)
+        w_raw = {}
+        for h in range(2):
+            for c in range(KP):
+                w_raw[c, h] = work.tile([P, 4, HALF], BF16, name="w_raw%d%d" % (c, h), tag="big", bufs=11, align_bytes=64)
+
+        def load_w(c, h):
+            nc.sync.dma_start(out=w_raw[c, h][:], in_=w_rows[c][:, :, h * HALF : (h + 1) * HALF])
+
+        proj_w = keep.tile([P, 2, 2 * R], U8, align_bytes=64)
+        pool_raw = keep.tile([P, 2, M], BF16, align_bytes=64)
+
+        def load_pos():
+            nc.sync.dma_start(out=pos[0:64], in_=space_pos.rearrange("(k t) d -> k t d", t=4))
+            nc.sync.dma_start(out=pos[64:72], in_=time_pos.unsqueeze(1).to_broadcast([T, 4, N]))
+
+        def load_gain():
+            nc.sync.dma_start(out=gain_bf[:], in_=gain.rearrange("(g p t) -> p g t", p=P, t=4))
+
+        def load_proj():
+            for q in range(4):
+                nc.sync.dma_start(
+                    out=proj_s[32 * q : 32 * q + 4].bitcast(I32),
+                    in_=proj_scales[:, 4 * q : 4 * q + 4, :].rearrange("g q n -> q g n").bitcast(I32),
+                )
+            nc.sync.dma_start(out=proj_w[:].bitcast(I32), in_=proj_words.rearrange("g p c -> p g c").bitcast(I32))
+
+        def load_pool():
+            nc.sync.dma_start(out=pool_raw[:], in_=pool.rearrange("(a p) m -> p a m", p=P))
+
+        loads = [
+            (DQ["x0a"], load_x, (0, slice(0, 1))), (DQ["x0b"], load_x, (0, slice(1, 2))),
+            (DQ["pos"], load_pos, ()), (DQ["gain"], load_gain, ()), (DQ["proj"], load_proj, ()), (DQ["pool"], load_pool, ()),
+        ]
+        for h in range(2):
+            for c in range(KP):
+                loads.append((DQ["w%d%d" % (c, h)], load_w, (c, h)))
+        for s in range(1, TILES // 2):
+            loads.append((DQ["x"] + s * 3, load_x, (s, slice(0, 2))))
+        for when, fn, args in sorted(loads, key=lambda x: x[0]):
+            fn(*args)
+
+        gain_f = keep.tile([P, TILES], F32, align_bytes=64)
+        sel = keep.tile([P, 4, 2, 64], BF16, align_bytes=64)
+        w_c = {}
+        w_s = {}
+        for h in range(2):
+            for c in range(KP):
+                w_c[c, h] = keep.tile([P, HALF], U32, name="w_c%d%d" % (c, h), align_bytes=64)
+                w_s[c, h] = keep.tile([P, HALF], U8, name="w_s%d%d" % (c, h), align_bytes=64)
+        h_c = []
+        h_s = []
+        for g in range(4):
+            h_c.append(keep.tile([P, N], U32, name="h_c%d" % g, align_bytes=64))
+            h_s.append(keep.tile([P, N], U8, name="h_s%d" % g, align_bytes=64))
+        p_c = keep.tile([P, 4, 2 * P], U32, align_bytes=64)
+        p_s = keep.tile([P, 4, 2 * P], U8, align_bytes=64)
+
+        xb = {}
+        xi = {}
+        xc = {}
+        xs = {}
+        pg = {}
+        hn = {}
+        hi = {}
+        hx = {}
+        hc = {}
+        hs = {}
+        wi = {}
+        ps_e = {}
+
+        def widen(i):
+            xb_t = work.tile([P, K], BF16, bufs=3, align_bytes=64)
+            xb[i] = xb_t
+            nc.vector.tensor_tensor(out=xb_t[:], in0=xr[i // 2][:, i % 2, :].bitcast(F8), in1=scale_bc[:], op=MULT)
+
+        def turn_x(i):
+            words = xb[i][:].bitcast(F32)
+            xi_t = work.tile([P, KP, P, 2], F32, bufs=3, align_bytes=64)
+            xi[i] = xi_t
+            for c0, nk in ((0, 2), (2, 1)):
+                ps_x = psum.tile([P, nk, 2, P], F32, bufs=2)
+                for c in range(nk):
+                    for u in range(2):
+                        k0 = 256 * (c0 + c)
+                        nc.tensor.transpose(ps_x[:, c, u, :], words[:, k0 + u : k0 + 256 : 2], ident[:])
+                nc.scalar.copy(out=xi_t[:, c0 : c0 + nk], in_=ps_x[:].rearrange("p c u m -> p c m u"))
+
+        def quantize_x(i):
+            xc_t = work.tile([P, KP, P], U32, bufs=3, align_bytes=64)
+            xs_t = work.tile([P, KP, P], U8, bufs=3, align_bytes=64)
+            xc[i] = xc_t
+            xs[i] = xs_t
+            for c0, nk in ((0, 2), (2, 1)):
+                cs = slice(c0, c0 + nk)
+                nc.vector.quantize_mx(
+                    out=xc_t[:, cs].rearrange("p c m -> p (c m)").bitcast(F8X4),
+                    scales=xs_t[:, cs].rearrange("p c m -> p (c m)"),
+                    in_=xi[i][:, cs].rearrange("p c m u -> p (c m u)").bitcast(BF16),
+                )
+
+        def group_w(c, h, eng):
+            wi_t = work.tile([P, HALF, 4], BF16, bufs=3, align_bytes=64)
+            wi[c, h] = wi_t
+            src = w_raw[c, h][:].rearrange("p j (q u e) -> p u q e j", u=2, e=2)
+            dst = wi_t[:].rearrange("p (u q e) j -> p u q e j", u=2, e=2)
+            for u in range(2):
+                if eng == "s":
+                    nc.scalar.copy(out=dst[:, u], in_=src[:, u])
+                else:
+                    nc.vector.tensor_copy(out=dst[:, u], in_=src[:, u])
+
+        def quantize_w(c, h):
+            nc.vector.quantize_mx(
+                out=w_c[c, h][:].bitcast(F8X4), scales=w_s[c, h][:], in_=wi[c, h][:].rearrange("p n j -> p (n j)")
+            )
+
+        def place(i, h):
+            g, t = i // 4, i % 4
+            if h == 0:
+                pg_t = work.tile([P, 2, HALF], F32, tag="big", bufs=11, align_bytes=64)
+                pg[i] = pg_t
+            ps_p = psum.tile([P, HALF], F32, bufs=1)
+            nc.tensor.matmul(
+                out=ps_p[:],
+                lhsT=sel[:, g].rearrange("p a b -> p (a b)"),
+                rhs=pos[:, t, h * HALF : (h + 1) * HALF],
+                start=True,
+                stop=True,
+            )
+            nc.scalar.activation(
+                out=pg[i][:, h].rearrange("p (u q e) -> p u q e", u=2, e=2),
+                in_=ps_p[:].rearrange("p (q u e) -> p u q e", u=2, e=2),
+                func=COPY,
+                scale=gain_f[:, i : i + 1],
+            )
+
+        def embed(i, h):
+            acc = psum.tile([P, HALF], F32, bufs=3)
+            ps_e[i, h] = acc
+            for c in range(KP):
+                nc.tensor.matmul_mx(
+                    out=acc[:],
+                    lhsT=xc[i][:, c].bitcast(F8X4),
+                    lhsT_scale=xs[i][:, c],
+                    rhs=w_c[c, h][:].bitcast(F8X4),
+                    rhs_scale=w_s[c, h][:],
+                    start=(c == 0),
+                    stop=(c == KP - 1),
+                )
+
+        def finish_h(i, h):
+            g, t = i // 4, i % 4
+            if t == 0 and h == 0:
+                hn_t = work.tile([P, 4, N], BF16, bufs=2, align_bytes=64)
+                hn[g] = hn_t
+            nc.vector.scalar_tensor_tensor(
+                out=hn[g][:, t, h * HALF : (h + 1) * HALF],
+                in0=ps_e[i, h][:],
+                scalar=gain_f[:, i : i + 1],
+                in1=pg[i][:, h],
+                op0=MULT,
+                op1=ADD,
+            )
+
+        def turn_h(i):
+            g, t = i // 4, i % 4
+            words = hn[g][:].rearrange("p t d -> p (t d)").bitcast(F32)
+            ps_h = psum.tile([P, 2, 2, P], F32, bufs=1)
+            for b in range(2):
+                for u in range(2):
+                    d0 = t * HALF + 256 * b + 128 * u
+                    nc.tensor.transpose(ps_h[:, b, u, :], words[:, d0 : d0 + 128], ident[:])
+            hx_t = work.tile([P, 2, P, 2], F32, bufs=3, align_bytes=64)
+            hx[i] = hx_t
+            nc.scalar.copy(out=hx_t[:], in_=ps_h[:].rearrange("p b u m -> p b m u"))
+
+        def quantize_hx(i):
+            hc_t = work.tile([P, 2, P], U32, bufs=2, align_bytes=64)
+            hs_t = work.tile([P, 2, P], U8, bufs=2, align_bytes=64)
+            hc[i] = hc_t
+            hs[i] = hs_t
+            nc.vector.quantize_mx(
+                out=hc_t[:].rearrange("p b m -> p (b m)").bitcast(F8X4),
+                scales=hs_t[:].rearrange("p b m -> p (b m)"),
+                in_=hx[i][:].rearrange("p b m u -> p (b m u)").bitcast(BF16),
+            )
+
+        def feats(i):
+            g, t = i // 4, i % 4
+            ps_f = psum.tile([P, R], F32, bufs=1)
+            for b in range(2):
+                nc.tensor.matmul_mx(
+                    out=ps_f[:],
+                    lhsT=hc[i][:, b].bitcast(F8X4),
+                    lhsT_scale=hs[i][:, b],
+                    rhs=proj_w[:, b].bitcast(F4X4),
+                    rhs_scale=proj_s[:, b],
+                    start=(b == 0),
+                    stop=(b == 1),
+                )
+            fo = work.tile([P, R], F32, bufs=3, align_bytes=64)
+            nc.scalar.copy(out=fo[:], in_=ps_f[:])
+            nc.sync.dma_start(out=out_0.rearrange("(g p t) r -> g t p r", p=P, t=4)[g, t], in_=fo[:])
+
+        def group_h(g, c, eng):
+            hi_t = work.tile([P, CH, 4], BF16, bufs=3, align_bytes=64)
+            hi[g, c] = hi_t
+            src = hn[g][:, :, c * CH : (c + 1) * CH].rearrange("p t d -> p d t")
+            if eng == "s":
+                nc.scalar.copy(out=hi_t[:], in_=src)
+            else:
+                nc.vector.tensor_copy(out=hi_t[:], in_=src)
+
+        def quantize_h(g, c):
+            ds = slice(c * CH, (c + 1) * CH)
+            nc.vector.quantize_mx(
+                out=h_c[g][:, ds].bitcast(F8X4), scales=h_s[g][:, ds], in_=hi[g, c][:].rearrange("p d t -> p (d t)")
+            )
+
+        pi = {}
+
+        def turn_pool(g):
+            words = pool_raw[:].rearrange("p a m -> p (a m)").bitcast(F32)
+            ps_h = psum.tile([P, 2, 2, P], F32, bufs=1)
+            for a in range(2):
+                for u in range(2):
+                    m0 = a * (M // 2) + 256 * g
+                    nc.tensor.transpose(ps_h[:, a, u, :], words[:, m0 + u : m0 + 256 : 2], ident[:])
+            pi_t = work.tile([P, 2, P, 2], F32, bufs=2, align_bytes=64)
+            pi[g] = pi_t
+            nc.scalar.copy(out=pi_t[:], in_=ps_h[:].rearrange("p a u l -> p a l u"))
+
+        def quantize_pool(g):
+            nc.vector.quantize_mx(
+                out=p_c[:, g].bitcast(F8X4),
+                scales=p_s[:, g],
+                in_=pi[g][:].rearrange("p a l u -> p (a l u)").bitcast(BF16),
+            )
+
+        def cast_gain():
+            nc.vector.tensor_copy(out=gain_f[:], in_=gain_bf[:].rearrange("p g t -> p (g t)"))
+
+        for g in range(4):
+            nc.vector.tensor_tensor(
+                out=sel[:, g],
+                in0=ident[:, 0:64].unsqueeze(1).to_broadcast([P, 2, 64]),
+                in1=ident[:, 64 + 2 * g : 66 + 2 * g].unsqueeze(2).to_broadcast([P, 2, 64]),
+                op=ADD,
+            )
+        acc = {}
+
+        def pool_pass(g, a, h):
+            if g == 0:
+                if a == 0:
+                    ps_x = psum.tile([P, HALF], F32, bufs=2)
+                    acc[a, h] = ps_x
+                elif h == 0:
+                    ps_p = psum.tile([P, HALF], F32, bufs=1)
+                    acc[a, h] = ps_p
+                else:
+                    ps_l = psum.tile([P, HALF], F32, tag="acc", bufs=3)
+                    acc[a, h] = ps_l
+            nc.tensor.matmul_mx(
+                out=acc[a, h][:],
+                lhsT=p_c[:, g, a * P : (a + 1) * P].bitcast(F8X4),
+                lhsT_scale=p_s[:, g, a * P : (a + 1) * P],
+                rhs=h_c[g][:, h * HALF : (h + 1) * HALF].bitcast(F8X4),
+                rhs_scale=h_s[g][:, h * HALF : (h + 1) * HALF],
+                start=(g == 0),
+                stop=(g == 3),
+            )
+
+        def latents_out(a, h):
+            lo = work.tile([P, HALF], F32, bufs=4, align_bytes=64)
+            src = acc[a, h][:].rearrange("p (u q e) -> p q u e", u=2, e=2)
+            dst = lo[:].rearrange("p (q u e) -> p q u e", u=2, e=2)
+            if a == 0:
+                nc.vector.tensor_copy(out=dst, in_=src)
+            else:
+                nc.scalar.copy(out=dst, in_=src)
+            nc.sync.dma_start(out=out_1[a * P : (a + 1) * P, h * HALF : (h + 1) * HALF], in_=lo[:])
+
+        plan = []
+
+        def at(when, fn, *args):
+            plan.append((when, len(plan), fn, args))
+
+        for i in range(TILES):
+            at(i + AT["widen"], widen, i)
+            at(i + AT["turn_x"], turn_x, i)
+            at(i + AT["quantize_x"], quantize_x, i)
+            for h in range(2):
+                at(i * AT["place_rate"] + AT["place%d" % h], place, i, h)
+                at(i + AT["embed%d" % h], embed, i, h)
+                at(i + AT["finish%d" % h], finish_h, i, h)
+            at(i + AT["turn_h"], turn_h, i)
+            at(i + AT["quantize_hx"], quantize_hx, i)
+            at(i + AT["feats"], feats, i)
+        at(AT["gain"], cast_gain)
+        for g in range(4):
+            at(AT["pool0"] + g * AT["pool_step"], turn_pool, g)
+            at(AT["pool0"] + g * AT["pool_step"] + AT["pool_q"], quantize_pool, g)
+            for c in range(4):
+                e = "s" if H_ON_S[4 * g + c] else "v"
+                if g < 3:
+                    at(4 * g + AT["group_h"] + c * AT["group_step"], group_h, g, c, e)
+                    at(4 * g + AT["quantize_h"] + c * AT["group_step"], quantize_h, g, c)
+                else:
+                    at(4 * g + AT["last_group"] + c * AT["last_step"], group_h, g, c, e)
+                    at(4 * g + AT["last_quantize"] + c * AT["last_step"], quantize_h, g, c)
+        for h in range(2):
+            for c in range(KP):
+                e = "s" if ON_S["wi%d%d" % (c, h)] else "v"
+                at(AT["wi%d%d" % (c, h)], group_w, c, h, e)
+                at(AT["wq%d%d" % (c, h)], quantize_w, c, h)
+        for g in range(3):
+            for h in range(2):
+                for a in range(2):
+                    at(AT["latents"], pool_pass, g, a, h)
+        end = 12 + AT["last_quantize"] + 3 * AT["last_step"] + 0.01
+        for h in range(2):
+            for a in range(2):
+                at(end if h else end - 2 * AT["last_step"], pool_pass, 3, a, h)
+                at(end + 10, latents_out, a, h)
+        for when, n, fn, args in sorted(plan, key=lambda x: (x[0], x[1])):
+            fn(*args)

@@ -23,11 +23,13 @@ KP = K // 512
 TILES = M // P
 HALF = 512
 CH = 256
+EARLY = 2
+BX, BH, BE, BF, BP = 2, 2, 2, 1, 1
 
-AT = {"widen":-1.8674,"turn_x":-1.6039,"quantize_x":-0.6549,"place0":-1.3658,"place1":-0.736,"embed0":-0.4106,"embed1":0.1152,"finish0":0.3843,"finish1":0.4498,"turn_h":1.1697,"quantize_hx":1.5792,"feats":2.2412,"group_h":5.151,"group_step":0.9683,"quantize_h":6.0619,"last_group":3.4646,"last_step":1.013,"last_quantize":5.1494,"pool0":3.3997,"pool_step":2.0081,"pool_q":0.9988,"wi00":-4.1691,"wi10":-2.4974,"wi20":-3.889,"wq00":-2.7189,"wq10":-1.6576,"wq20":-1.2366,"wi01":-0.8594,"wi11":-1.6815,"wi21":-0.9131,"wq01":0.0682,"wq11":0.0603,"wq21":-0.6822,"latents":17.205,"gain":-1.858,"place_rate":0.9955}
-DQ = {"x0a":-0.5647,"w00":-4.2437,"w10":-3.1927,"x0b":0.4036,"w20":-3.3619,"gain":-5.1961,"pos":2.7926,"w01":8.9419,"w11":0.6852,"w21":2.3029,"x":7.2407,"proj":22.0402,"pool":11.5476}
-ON_S = {"wi00":0,"wi10":1,"wi20":0,"wi01":1,"wi11":1,"wi21":0}
-H_ON_S = [0,0,1,0,1,0,1,1,0,0,1,1,0,0,0,0]
+AT = {"widen":-1.6391,"turn_x0":-1.2984,"turn_x1":-1.2119,"empty_x0":-0.995,"empty_x1":-0.5874,"quantize_x0":-0.3613,"quantize_x1":-0.1584,"place_rate":0.987,"place0":-0.91,"empty_p0":-0.711,"place1":-0.3766,"empty_p1":-0.1477,"embed0":0.2458,"embed1":0.2459,"finish0":0.4717,"finish1":0.676,"turn_h":0.8043,"empty_h":1.4542,"quantize_hx":2.2959,"feats":2.5942,"empty_f":2.9205,"gain":-26.5487,"pool_e":1.1593,"pool_q":5.8406,"group_h":4.6791,"group_step":1.0077,"quantize_h":6.906,"last_g0":23.5427,"last_q0":24.9872,"last_g1":16.2916,"last_q1":16.5845,"last_g2":24.1745,"last_q2":26.8415,"last_g3":17.5422,"last_q3":28.2572,"wi00":-42.8617,"wi10":-94.4186,"wi20":-31.8169,"wq00":-5.4876,"wq10":-92.8545,"wq20":-18.6131,"wi01":-19.4771,"wi11":-60.2055,"wi21":-55.4042,"wq01":-18.1206,"wq11":-47.5607,"wq21":-28.2244,"lat0":16.4447,"lat1":17.2994,"lat2":25.1366,"lat30":25.4624,"lat31":28.5219,"pool_t0":-2.5396,"pool_t1":-1.0824,"pool_t2":15.7353,"pool_t3":-2.0343,"late0":-0.2036,"late1":-0.1272,"late2":0.0389,"odd_widen":-0.2658,"odd_turn_x0":-0.091,"odd_turn_x1":-0.1887,"odd_empty_x0":0.2218,"odd_empty_x1":-0.3905,"odd_quantize_x0":-0.053,"odd_quantize_x1":-0.0884,"odd_place0":0.1425,"odd_place1":0.0622,"odd_empty_p0":0.3015,"odd_empty_p1":0.0922,"odd_embed0":-0.1122,"odd_embed1":0.0234,"odd_finish0":-0.1526,"odd_finish1":-0.139,"odd_turn_h":0.0955,"odd_empty_h":0.4252,"odd_quantize_hx":-0.1326,"odd_feats":-0.0165,"odd_empty_f":-0.0013}
+DQ = {"x0a":-3.9746,"w00":-18.7586,"w10":-86.2992,"x0b":45.7335,"w20":-41.6683,"gain":-24.4198,"pos":47.2604,"w01":23.7696,"w11":-41.8239,"w21":-73.4278,"scale":53.3079,"x":48.4335,"proj":56.0165,"pool":43.9633}
+ON_S = {"wi00":0,"wi10":0,"wi20":1,"wi01":0,"wi11":0,"wi21":1}
+H_ON_S = [1,1,1,0,1,1,1,0,1,0,1,1,0,0,0,1]
 
 
 def tile_tubelet_embed_pool_s8_kernel(
@@ -41,7 +43,8 @@ def tile_tubelet_embed_pool_s8_kernel(
         ctx.enter_context(tc.manual_schedule())
 
         scale_bc = keep.tile([P, K], F32, align_bytes=64)
-        nc.scalar.dma_start(out=scale_bc[:], in_=x_scale.rearrange("o k -> (o k)").partition_broadcast(P))
+        scale_k = keep.tile([P, KP, 4], F32)
+        nc.scalar.dma_start(out=scale_k[:], in_=x_scale.rearrange("o (c p t) -> p (o c) t", p=P, t=4))
         gain_bf = keep.tile([P, 4, 4], BF16)
 
         ident = keep.tile([P, P], F32, align_bytes=64)
@@ -76,6 +79,9 @@ def tile_tubelet_embed_pool_s8_kernel(
             nc.sync.dma_start(out=pos[0:64], in_=space_pos.rearrange("(k t) d -> k t d", t=4))
             nc.sync.dma_start(out=pos[64:72], in_=time_pos.unsqueeze(1).to_broadcast([T, 4, N]))
 
+        def load_scale():
+            nc.sync.dma_start(out=scale_bc[:], in_=x_scale.rearrange("o k -> (o k)").partition_broadcast(P))
+
         def load_gain():
             nc.sync.dma_start(out=gain_bf[:], in_=gain.rearrange("(g p t) -> p g t", p=P, t=4))
 
@@ -92,7 +98,7 @@ def tile_tubelet_embed_pool_s8_kernel(
 
         loads = [
             (DQ["x0a"], load_x, (0, slice(0, 1))), (DQ["x0b"], load_x, (0, slice(1, 2))),
-            (DQ["pos"], load_pos, ()), (DQ["gain"], load_gain, ()), (DQ["proj"], load_proj, ()), (DQ["pool"], load_pool, ()),
+            (DQ["pos"], load_pos, ()), (DQ["scale"], load_scale, ()), (DQ["gain"], load_gain, ()), (DQ["proj"], load_proj, ()), (DQ["pool"], load_pool, ()),
         ]
         for h in range(2):
             for c in range(KP):
@@ -130,36 +136,60 @@ def tile_tubelet_embed_pool_s8_kernel(
         hs = {}
         wi = {}
         ps_e = {}
+        px = {}
+        pp = {}
+        ph = {}
+        pf = {}
 
         def widen(i):
             xb_t = work.tile([P, K], BF16, bufs=3, align_bytes=64)
             xb[i] = xb_t
-            nc.vector.tensor_tensor(out=xb_t[:], in0=xr[i // 2][:, i % 2, :].bitcast(F8), in1=scale_bc[:], op=MULT)
+            codes = xr[i // 2][:, i % 2, :].bitcast(F8)
+            if i < EARLY:
+                nc.scalar.copy(out=xb_t[:], in_=codes)
+            else:
+                nc.vector.tensor_tensor(out=xb_t[:], in0=codes, in1=scale_bc[:], op=MULT)
 
-        def turn_x(i):
+        banks = ((0, 2), (2, 1))
+
+        def turn_x(i, b):
             words = xb[i][:].bitcast(F32)
-            xi_t = work.tile([P, KP, P, 2], F32, bufs=3, align_bytes=64)
-            xi[i] = xi_t
-            for c0, nk in ((0, 2), (2, 1)):
-                ps_x = psum.tile([P, nk, 2, P], F32, bufs=2)
-                for c in range(nk):
-                    for u in range(2):
-                        k0 = 256 * (c0 + c)
-                        nc.tensor.transpose(ps_x[:, c, u, :], words[:, k0 + u : k0 + 256 : 2], ident[:])
-                nc.scalar.copy(out=xi_t[:, c0 : c0 + nk], in_=ps_x[:].rearrange("p c u m -> p c m u"))
+            c0, nk = banks[b]
+            if b == 0:
+                xi_t = work.tile([P, KP, P, 2], F32, bufs=3, align_bytes=64)
+                xi[i] = xi_t
+            ps_x = psum.tile([P, nk, 2, P], F32, bufs=BX)
+            px[i, b] = ps_x
+            for c in range(nk):
+                for u in range(2):
+                    k0 = 256 * (c0 + c)
+                    nc.tensor.transpose(ps_x[:, c, u, :], words[:, k0 + u : k0 + 256 : 2], ident[:])
 
-        def quantize_x(i):
-            xc_t = work.tile([P, KP, P], U32, bufs=3, align_bytes=64)
-            xs_t = work.tile([P, KP, P], U8, bufs=3, align_bytes=64)
-            xc[i] = xc_t
-            xs[i] = xs_t
-            for c0, nk in ((0, 2), (2, 1)):
-                cs = slice(c0, c0 + nk)
-                nc.vector.quantize_mx(
-                    out=xc_t[:, cs].rearrange("p c m -> p (c m)").bitcast(F8X4),
-                    scales=xs_t[:, cs].rearrange("p c m -> p (c m)"),
-                    in_=xi[i][:, cs].rearrange("p c m u -> p (c m u)").bitcast(BF16),
-                )
+        def empty_x(i, b):
+            c0, nk = banks[b]
+            if i >= EARLY:
+                nc.scalar.copy(out=xi[i][:, c0 : c0 + nk], in_=px[i, b][:].rearrange("p c u m -> p c m u"))
+                return
+            raw = px[i, b][:].rearrange("p c u m -> p (c u m)").bitcast(BF16)
+            raw = raw.rearrange("p (c u m e) -> p c m u e", c=nk, u=2, e=2)
+            dst = xi[i][:].rearrange("p c m u -> p (c m u)").bitcast(BF16)
+            dst = dst.rearrange("p (c m u e) -> p c m u e", c=KP, u=2, e=2)
+            for c in range(nk):
+                by = scale_k[:, c0 + c].rearrange("p (u e) -> p u e", u=2).unsqueeze(1).to_broadcast([P, P, 2, 2])
+                nc.vector.tensor_tensor(out=dst[:, c0 + c], in0=raw[:, c], in1=by, op=MULT)
+
+        def quantize_x(i, b):
+            if b == 0:
+                xc_t = work.tile([P, KP, P], U32, bufs=3, align_bytes=64)
+                xs_t = work.tile([P, KP, P], U8, bufs=3, align_bytes=64)
+                xc[i] = xc_t
+                xs[i] = xs_t
+            cs = slice(banks[b][0], sum(banks[b]))
+            nc.vector.quantize_mx(
+                out=xc[i][:, cs].rearrange("p c m -> p (c m)").bitcast(F8X4),
+                scales=xs[i][:, cs].rearrange("p c m -> p (c m)"),
+                in_=xi[i][:, cs].rearrange("p c m u -> p (c m u)").bitcast(BF16),
+            )
 
         def group_w(c, h, eng):
             wi_t = work.tile([P, HALF, 4], BF16, bufs=3, align_bytes=64)
@@ -182,7 +212,8 @@ def tile_tubelet_embed_pool_s8_kernel(
             if h == 0:
                 pg_t = work.tile([P, 2, HALF], F32, tag="big", bufs=11, align_bytes=64)
                 pg[i] = pg_t
-            ps_p = psum.tile([P, HALF], F32, bufs=1)
+            ps_p = psum.tile([P, HALF], F32, bufs=BP)
+            pp[i, h] = ps_p
             nc.tensor.matmul(
                 out=ps_p[:],
                 lhsT=sel[:, g].rearrange("p a b -> p (a b)"),
@@ -190,15 +221,17 @@ def tile_tubelet_embed_pool_s8_kernel(
                 start=True,
                 stop=True,
             )
+
+        def empty_p(i, h):
             nc.scalar.activation(
                 out=pg[i][:, h].rearrange("p (u q e) -> p u q e", u=2, e=2),
-                in_=ps_p[:].rearrange("p (q u e) -> p u q e", u=2, e=2),
+                in_=pp[i, h][:].rearrange("p (q u e) -> p u q e", u=2, e=2),
                 func=COPY,
                 scale=gain_f[:, i : i + 1],
             )
 
         def embed(i, h):
-            acc = psum.tile([P, HALF], F32, bufs=3)
+            acc = psum.tile([P, HALF], F32, bufs=BE)
             ps_e[i, h] = acc
             for c in range(KP):
                 nc.tensor.matmul_mx(
@@ -228,14 +261,17 @@ def tile_tubelet_embed_pool_s8_kernel(
         def turn_h(i):
             g, t = i // 4, i % 4
             words = hn[g][:].rearrange("p t d -> p (t d)").bitcast(F32)
-            ps_h = psum.tile([P, 2, 2, P], F32, bufs=1)
+            ps_h = psum.tile([P, 2, 2, P], F32, bufs=BH)
             for b in range(2):
                 for u in range(2):
                     d0 = t * HALF + 256 * b + 128 * u
                     nc.tensor.transpose(ps_h[:, b, u, :], words[:, d0 : d0 + 128], ident[:])
+            ph[i] = ps_h
+
+        def empty_h(i):
             hx_t = work.tile([P, 2, P, 2], F32, bufs=3, align_bytes=64)
             hx[i] = hx_t
-            nc.scalar.copy(out=hx_t[:], in_=ps_h[:].rearrange("p b u m -> p b m u"))
+            nc.scalar.copy(out=hx_t[:], in_=ph[i][:].rearrange("p b u m -> p b m u"))
 
         def quantize_hx(i):
             hc_t = work.tile([P, 2, P], U32, bufs=2, align_bytes=64)
@@ -250,7 +286,7 @@ def tile_tubelet_embed_pool_s8_kernel(
 
         def feats(i):
             g, t = i // 4, i % 4
-            ps_f = psum.tile([P, R], F32, bufs=1)
+            ps_f = psum.tile([P, R], F32, bufs=BF)
             for b in range(2):
                 nc.tensor.matmul_mx(
                     out=ps_f[:],
@@ -261,18 +297,23 @@ def tile_tubelet_embed_pool_s8_kernel(
                     start=(b == 0),
                     stop=(b == 1),
                 )
+            pf[i] = ps_f
+
+        def empty_f(i):
+            g, t = i // 4, i % 4
             fo = work.tile([P, R], F32, bufs=3, align_bytes=64)
-            nc.scalar.copy(out=fo[:], in_=ps_f[:])
+            nc.scalar.copy(out=fo[:], in_=pf[i][:])
             nc.sync.dma_start(out=out_0.rearrange("(g p t) r -> g t p r", p=P, t=4)[g, t], in_=fo[:])
 
         def group_h(g, c, eng):
             hi_t = work.tile([P, CH, 4], BF16, bufs=3, align_bytes=64)
             hi[g, c] = hi_t
-            src = hn[g][:, :, c * CH : (c + 1) * CH].rearrange("p t d -> p d t")
+            src = hn[g][:, :, c * CH : (c + 1) * CH].rearrange("p t (n i) -> p n t i", i=4)
+            dst = hi_t[:].rearrange("p (n i) t -> p n t i", i=4)
             if eng == "s":
-                nc.scalar.copy(out=hi_t[:], in_=src)
+                nc.scalar.copy(out=dst, in_=src)
             else:
-                nc.vector.tensor_copy(out=hi_t[:], in_=src)
+                nc.vector.tensor_copy(out=dst, in_=src)
 
         def quantize_h(g, c):
             ds = slice(c * CH, (c + 1) * CH)
@@ -284,14 +325,17 @@ def tile_tubelet_embed_pool_s8_kernel(
 
         def turn_pool(g):
             words = pool_raw[:].rearrange("p a m -> p (a m)").bitcast(F32)
-            ps_h = psum.tile([P, 2, 2, P], F32, bufs=1)
+            ps_h = psum.tile([P, 2, 2, P], F32, bufs=BH)
             for a in range(2):
                 for u in range(2):
                     m0 = a * (M // 2) + 256 * g
                     nc.tensor.transpose(ps_h[:, a, u, :], words[:, m0 + u : m0 + 256 : 2], ident[:])
-            pi_t = work.tile([P, 2, P, 2], F32, bufs=2, align_bytes=64)
+            ph["pool", g] = ps_h
+
+        def empty_pool(g):
+            pi_t = work.tile([P, 2, P, 2], F32, bufs=4, align_bytes=64)
             pi[g] = pi_t
-            nc.scalar.copy(out=pi_t[:], in_=ps_h[:].rearrange("p a u l -> p a l u"))
+            nc.scalar.copy(out=pi_t[:], in_=ph["pool", g][:].rearrange("p a u l -> p a l u"))
 
         def quantize_pool(g):
             nc.vector.quantize_mx(
@@ -315,13 +359,13 @@ def tile_tubelet_embed_pool_s8_kernel(
         def pool_pass(g, a, h):
             if g == 0:
                 if a == 0:
-                    ps_x = psum.tile([P, HALF], F32, bufs=2)
+                    ps_x = psum.tile([P, HALF], F32, bufs=BX)
                     acc[a, h] = ps_x
                 elif h == 0:
-                    ps_p = psum.tile([P, HALF], F32, bufs=1)
+                    ps_p = psum.tile([P, HALF], F32, bufs=BP)
                     acc[a, h] = ps_p
                 else:
-                    ps_l = psum.tile([P, HALF], F32, tag="acc", bufs=3)
+                    ps_l = psum.tile([P, HALF], F32, tag="acc", bufs=BE)
                     acc[a, h] = ps_l
             nc.tensor.matmul_mx(
                 out=acc[a, h][:],
@@ -349,41 +393,47 @@ def tile_tubelet_embed_pool_s8_kernel(
             plan.append((when, len(plan), fn, args))
 
         for i in range(TILES):
-            at(i + AT["widen"], widen, i)
-            at(i + AT["turn_x"], turn_x, i)
-            at(i + AT["quantize_x"], quantize_x, i)
+
+            def stage(key, fn, *args, rate=1.0, late=0):
+                at(i * rate + late + AT[key] + (i % 2) * AT["odd_" + key], fn, *args)
+
+            stage("widen", widen, i)
             for h in range(2):
-                at(i * AT["place_rate"] + AT["place%d" % h], place, i, h)
-                at(i + AT["embed%d" % h], embed, i, h)
-                at(i + AT["finish%d" % h], finish_h, i, h)
-            at(i + AT["turn_h"], turn_h, i)
-            at(i + AT["quantize_hx"], quantize_hx, i)
-            at(i + AT["feats"], feats, i)
+                stage("turn_x%d" % h, turn_x, i, h)
+                stage("empty_x%d" % h, empty_x, i, h)
+                stage("quantize_x%d" % h, quantize_x, i, h)
+                stage("place%d" % h, place, i, h, rate=AT["place_rate"])
+                stage("empty_p%d" % h, empty_p, i, h, rate=AT["place_rate"])
+                late = h * AT["late%d" % i] if i < 3 else 0
+                stage("embed%d" % h, embed, i, h, late=late)
+                stage("finish%d" % h, finish_h, i, h, late=late)
+            stage("turn_h", turn_h, i)
+            stage("empty_h", empty_h, i)
+            stage("quantize_hx", quantize_hx, i)
+            stage("feats", feats, i)
+            stage("empty_f", empty_f, i)
         at(AT["gain"], cast_gain)
         for g in range(4):
-            at(AT["pool0"] + g * AT["pool_step"], turn_pool, g)
-            at(AT["pool0"] + g * AT["pool_step"] + AT["pool_q"], quantize_pool, g)
+            at(AT["pool_t%d" % g], turn_pool, g)
+            at(AT["pool_t%d" % g] + AT["pool_e"], empty_pool, g)
+            at(AT["pool_t%d" % g] + AT["pool_q"], quantize_pool, g)
             for c in range(4):
                 e = "s" if H_ON_S[4 * g + c] else "v"
                 if g < 3:
-                    at(4 * g + AT["group_h"] + c * AT["group_step"], group_h, g, c, e)
-                    at(4 * g + AT["quantize_h"] + c * AT["group_step"], quantize_h, g, c)
+                    at(4 * g + c * AT["group_step"] + AT["group_h"], group_h, g, c, e)
+                    at(4 * g + c * AT["group_step"] + AT["quantize_h"], quantize_h, g, c)
                 else:
-                    at(4 * g + AT["last_group"] + c * AT["last_step"], group_h, g, c, e)
-                    at(4 * g + AT["last_quantize"] + c * AT["last_step"], quantize_h, g, c)
+                    at(AT["last_g%d" % c], group_h, g, c, e)
+                    at(AT["last_q%d" % c], quantize_h, g, c)
         for h in range(2):
             for c in range(KP):
                 e = "s" if ON_S["wi%d%d" % (c, h)] else "v"
                 at(AT["wi%d%d" % (c, h)], group_w, c, h, e)
                 at(AT["wq%d%d" % (c, h)], quantize_w, c, h)
-        for g in range(3):
-            for h in range(2):
-                for a in range(2):
-                    at(AT["latents"], pool_pass, g, a, h)
-        end = 12 + AT["last_quantize"] + 3 * AT["last_step"] + 0.01
         for h in range(2):
             for a in range(2):
-                at(end if h else end - 2 * AT["last_step"], pool_pass, 3, a, h)
-                at(end + 10, latents_out, a, h)
+                for g in range(4):
+                    at(AT["lat%d" % g] if g < 3 else AT["lat3%d" % h], pool_pass, g, a, h)
+                at(30 + h, latents_out, a, h)
         for when, n, fn, args in sorted(plan, key=lambda x: (x[0], x[1])):
             fn(*args)

@@ -24,12 +24,13 @@ TILES = M // P
 HALF = 512
 CH = 256
 EARLY = 2
+TAIL = ("embed0", "embed1", "finish0", "finish1", "turn_h", "empty_h", "quantize_hx", "feats", "empty_f")
 BX, BH, BE, BF, BP = 2, 2, 2, 1, 1
 
-AT = {"widen":-1.6391,"turn_x0":-1.2984,"turn_x1":-1.2119,"empty_x0":-0.995,"empty_x1":-0.5874,"quantize_x0":-0.3613,"quantize_x1":-0.1584,"place_rate":0.987,"place0":-0.91,"empty_p0":-0.711,"place1":-0.3766,"empty_p1":-0.1477,"embed0":0.2458,"embed1":0.2459,"finish0":0.4717,"finish1":0.676,"turn_h":0.8043,"empty_h":1.4542,"quantize_hx":2.2959,"feats":2.5942,"empty_f":2.9205,"gain":-26.5487,"pool_e":1.1593,"pool_q":5.8406,"group_h":4.6791,"group_step":1.0077,"quantize_h":6.906,"last_g0":23.5427,"last_q0":24.9872,"last_g1":16.2916,"last_q1":16.5845,"last_g2":24.1745,"last_q2":26.8415,"last_g3":17.5422,"last_q3":28.2572,"wi00":-42.8617,"wi10":-94.4186,"wi20":-31.8169,"wq00":-5.4876,"wq10":-92.8545,"wq20":-18.6131,"wi01":-19.4771,"wi11":-60.2055,"wi21":-55.4042,"wq01":-18.1206,"wq11":-47.5607,"wq21":-28.2244,"lat0":16.4447,"lat1":17.2994,"lat2":25.1366,"lat30":25.4624,"lat31":28.5219,"pool_t0":-2.5396,"pool_t1":-1.0824,"pool_t2":15.7353,"pool_t3":-2.0343,"late0":-0.2036,"late1":-0.1272,"late2":0.0389,"odd_widen":-0.2658,"odd_turn_x0":-0.091,"odd_turn_x1":-0.1887,"odd_empty_x0":0.2218,"odd_empty_x1":-0.3905,"odd_quantize_x0":-0.053,"odd_quantize_x1":-0.0884,"odd_place0":0.1425,"odd_place1":0.0622,"odd_empty_p0":0.3015,"odd_empty_p1":0.0922,"odd_embed0":-0.1122,"odd_embed1":0.0234,"odd_finish0":-0.1526,"odd_finish1":-0.139,"odd_turn_h":0.0955,"odd_empty_h":0.4252,"odd_quantize_hx":-0.1326,"odd_feats":-0.0165,"odd_empty_f":-0.0013}
-DQ = {"x0a":-3.9746,"w00":-18.7586,"w10":-86.2992,"x0b":45.7335,"w20":-41.6683,"gain":-24.4198,"pos":47.2604,"w01":23.7696,"w11":-41.8239,"w21":-73.4278,"scale":53.3079,"x":48.4335,"proj":56.0165,"pool":43.9633}
+AT = {"widen":-1.6661,"turn_x0":-1.2984,"turn_x1":-1.2119,"empty_x0":-1.0101,"empty_x1":-0.6513,"quantize_x0":-0.3643,"quantize_x1":-0.1772,"place_rate":0.987,"place0":-0.9391,"empty_p0":-0.831,"place1":-0.3766,"empty_p1":-0.1477,"embed0":0.2334,"embed1":0.2454,"finish0":0.4819,"finish1":0.7016,"turn_h":0.8043,"empty_h":1.4335,"quantize_hx":2.2604,"feats":2.5783,"empty_f":2.9516,"gain":-26.8658,"pool_e":1.1475,"pool_q":6.3119,"group_h":4.6791,"group_step":1.0255,"quantize_h":5.9181,"last_g0":24.4784,"last_q0":24.9828,"last_g1":16.1959,"last_q1":17.6439,"last_g2":24.6936,"last_q2":25.5994,"last_g3":17.4967,"last_q3":28.5963,"wi00":-42.7302,"wi10":-93.9649,"wi20":-31.6716,"wq00":-4.7449,"wq10":-92.5035,"wq20":-18.4022,"wi01":-19.7062,"wi11":-60.1055,"wi21":-55.3939,"wq01":-17.7062,"wq11":-47.5256,"wq21":-28.2922,"lat0":16.1972,"lat1":17.2217,"lat2":25.1911,"lat30":25.8096,"lat31":29.9634,"pool_t0":-2.5827,"pool_t1":-0.9694,"pool_t2":15.6612,"pool_t3":-2.0304,"late0":-0.0046,"late1":0.1249,"late2":0.0425,"odd_widen":-0.2474,"odd_turn_x0":-0.091,"odd_turn_x1":-0.1891,"odd_empty_x0":0.2051,"odd_empty_x1":-0.2995,"odd_quantize_x0":0.1294,"odd_quantize_x1":0.2566,"odd_place0":0.1929,"odd_place1":0.0622,"odd_empty_p0":0.3089,"odd_empty_p1":0.0933,"odd_embed0":-0.0626,"odd_embed1":0.1718,"odd_finish0":-0.1526,"odd_finish1":-0.0912,"odd_turn_h":0.0341,"odd_empty_h":0.4252,"odd_quantize_hx":-0.1274,"odd_feats":-0.0392,"odd_empty_f":-0.0168,"tail_embed0_14":-0.0609,"tail_embed0_15":0.0339,"tail_embed1_14":0.1319,"tail_embed1_15":0.1135,"tail_finish0_14":0.049,"tail_finish0_15":-0.104,"tail_finish1_14":-0.1521,"tail_finish1_15":0.0239,"tail_turn_h_14":0.2957,"tail_turn_h_15":0.0366,"tail_empty_h_14":-0.1201,"tail_empty_h_15":-0.3125,"tail_quantize_hx_14":-0.181,"tail_quantize_hx_15":0.0335,"tail_feats_14":0.177,"tail_feats_15":-0.0273,"tail_empty_f_14":0.2037,"tail_empty_f_15":0.0285,"lo00":-0.038,"lo01":1.1097,"lo10":0.1455,"lo11":1.2804}
+DQ = {"x0a":-4.512,"w00":-17.1473,"w10":-86.2143,"x0b":46.2804,"w20":-41.6917,"gain":24.0272,"pos":46.8802,"w01":24.0172,"w11":-42.0443,"w21":-72.8333,"scale":53.9738,"x":47.9936,"proj":55.8693,"pool":44.2499}
 ON_S = {"wi00":0,"wi10":0,"wi20":1,"wi01":0,"wi11":0,"wi21":1}
-H_ON_S = [1,1,1,0,1,1,1,0,1,0,1,1,0,0,0,1]
+H_ON_S = [0,1,1,0,1,1,1,0,1,0,1,1,0,0,0,1]
 
 
 def tile_tubelet_embed_pool_s8_kernel(
@@ -155,7 +156,7 @@ def tile_tubelet_embed_pool_s8_kernel(
         def turn_x(i, b):
             words = xb[i][:].bitcast(F32)
             c0, nk = banks[b]
-            if b == 0:
+            if i not in xi:
                 xi_t = work.tile([P, KP, P, 2], F32, bufs=3, align_bytes=64)
                 xi[i] = xi_t
             ps_x = psum.tile([P, nk, 2, P], F32, bufs=BX)
@@ -179,7 +180,7 @@ def tile_tubelet_embed_pool_s8_kernel(
                 nc.vector.tensor_tensor(out=dst[:, c0 + c], in0=raw[:, c], in1=by, op=MULT)
 
         def quantize_x(i, b):
-            if b == 0:
+            if i not in xc:
                 xc_t = work.tile([P, KP, P], U32, bufs=3, align_bytes=64)
                 xs_t = work.tile([P, KP, P], U8, bufs=3, align_bytes=64)
                 xc[i] = xc_t
@@ -194,13 +195,12 @@ def tile_tubelet_embed_pool_s8_kernel(
         def group_w(c, h, eng):
             wi_t = work.tile([P, HALF, 4], BF16, bufs=3, align_bytes=64)
             wi[c, h] = wi_t
-            src = w_raw[c, h][:].rearrange("p j (q u e) -> p u q e j", u=2, e=2)
-            dst = wi_t[:].rearrange("p (u q e) j -> p u q e j", u=2, e=2)
-            for u in range(2):
-                if eng == "s":
-                    nc.scalar.copy(out=dst[:, u], in_=src[:, u])
-                else:
-                    nc.vector.tensor_copy(out=dst[:, u], in_=src[:, u])
+            src = w_raw[c, h][:].rearrange("p j (q u e) -> p q j u e", u=2, e=2)
+            dst = wi_t[:].rearrange("p (u q e) j -> p q j u e", u=2, e=2)
+            if eng == "s":
+                nc.scalar.copy(out=dst, in_=src)
+            else:
+                nc.vector.tensor_copy(out=dst, in_=src)
 
         def quantize_w(c, h):
             nc.vector.quantize_mx(
@@ -209,7 +209,7 @@ def tile_tubelet_embed_pool_s8_kernel(
 
         def place(i, h):
             g, t = i // 4, i % 4
-            if h == 0:
+            if i not in pg:
                 pg_t = work.tile([P, 2, HALF], F32, tag="big", bufs=11, align_bytes=64)
                 pg[i] = pg_t
             ps_p = psum.tile([P, HALF], F32, bufs=BP)
@@ -246,7 +246,7 @@ def tile_tubelet_embed_pool_s8_kernel(
 
         def finish_h(i, h):
             g, t = i // 4, i % 4
-            if t == 0 and h == 0:
+            if g not in hn:
                 hn_t = work.tile([P, 4, N], BF16, bufs=2, align_bytes=64)
                 hn[g] = hn_t
             nc.vector.scalar_tensor_tensor(
@@ -357,7 +357,7 @@ def tile_tubelet_embed_pool_s8_kernel(
         acc = {}
 
         def pool_pass(g, a, h):
-            if g == 0:
+            if (a, h) not in acc:
                 if a == 0:
                     ps_x = psum.tile([P, HALF], F32, bufs=BX)
                     acc[a, h] = ps_x
@@ -395,20 +395,22 @@ def tile_tubelet_embed_pool_s8_kernel(
         for i in range(TILES):
 
             def stage(key, fn, *args, rate=1.0, late=0):
+                if i >= 14 and key in TAIL:
+                    late = late + AT["tail_%s_%d" % (key, i)]
                 at(i * rate + late + AT[key] + (i % 2) * AT["odd_" + key], fn, *args)
 
             stage("widen", widen, i)
+            early = AT["late%d" % i] if i < 3 else 0
             for h in range(2):
                 stage("turn_x%d" % h, turn_x, i, h)
                 stage("empty_x%d" % h, empty_x, i, h)
                 stage("quantize_x%d" % h, quantize_x, i, h)
                 stage("place%d" % h, place, i, h, rate=AT["place_rate"])
                 stage("empty_p%d" % h, empty_p, i, h, rate=AT["place_rate"])
-                late = h * AT["late%d" % i] if i < 3 else 0
-                stage("embed%d" % h, embed, i, h, late=late)
-                stage("finish%d" % h, finish_h, i, h, late=late)
-            stage("turn_h", turn_h, i)
-            stage("empty_h", empty_h, i)
+                stage("embed%d" % h, embed, i, h, late=h * early)
+                stage("finish%d" % h, finish_h, i, h, late=h * early)
+            stage("turn_h", turn_h, i, late=early)
+            stage("empty_h", empty_h, i, late=early)
             stage("quantize_hx", quantize_hx, i)
             stage("feats", feats, i)
             stage("empty_f", empty_f, i)
@@ -434,6 +436,6 @@ def tile_tubelet_embed_pool_s8_kernel(
             for a in range(2):
                 for g in range(4):
                     at(AT["lat%d" % g] if g < 3 else AT["lat3%d" % h], pool_pass, g, a, h)
-                at(30 + h, latents_out, a, h)
+                at(30 + AT["lo%d%d" % (a, h)], latents_out, a, h)
         for when, n, fn, args in sorted(plan, key=lambda x: (x[0], x[1])):
             fn(*args)

@@ -3,7 +3,7 @@ from contextlib import ExitStack
 import concourse.mybir as mybir
 from concourse.masks import make_identity
 
-M, T, S, K, N, R, L = 2048, 8, 256, 1536, 1024, 512, 256
+M, T, K, N, R, L = 2048, 8, 1536, 1024, 512, 256
 FLOPS = 2 * (M * K * N + M * N * R + L * M * N)
 
 F32 = mybir.dt.float32
@@ -19,18 +19,14 @@ ADD = mybir.AluOpType.add
 MULT = mybir.AluOpType.mult
 
 P = 128
-KP = K // 512
+PASSES = K // 512
+GROUPS = M // 512
 TILES = M // P
 HALF = 512
-CH = 256
-EARLY = 2
-TAIL = ("embed0", "embed1", "finish0", "finish1", "turn_h", "empty_h", "quantize_hx", "feats", "empty_f")
-BX, BH, BE, BF, BP = 2, 2, 2, 1, 1
-
-AT = {"widen":-1.6661,"turn_x0":-1.2984,"turn_x1":-1.2119,"empty_x0":-1.0101,"empty_x1":-0.6513,"quantize_x0":-0.3643,"quantize_x1":-0.1772,"place_rate":0.987,"place0":-0.9391,"empty_p0":-0.831,"place1":-0.3766,"empty_p1":-0.1477,"embed0":0.2334,"embed1":0.2454,"finish0":0.4819,"finish1":0.7016,"turn_h":0.8043,"empty_h":1.4335,"quantize_hx":2.2604,"feats":2.5783,"empty_f":2.9516,"gain":-26.8658,"pool_e":1.1475,"pool_q":6.3119,"group_h":4.6791,"group_step":1.0255,"quantize_h":5.9181,"last_g0":24.4784,"last_q0":24.9828,"last_g1":16.1959,"last_q1":17.6439,"last_g2":24.6936,"last_q2":25.5994,"last_g3":17.4967,"last_q3":28.5963,"wi00":-42.7302,"wi10":-93.9649,"wi20":-31.6716,"wq00":-4.7449,"wq10":-92.5035,"wq20":-18.4022,"wi01":-19.7062,"wi11":-60.1055,"wi21":-55.3939,"wq01":-17.7062,"wq11":-47.5256,"wq21":-28.2922,"lat0":16.1972,"lat1":17.2217,"lat2":25.1911,"lat30":25.8096,"lat31":29.9634,"pool_t0":-2.5827,"pool_t1":-0.9694,"pool_t2":15.6612,"pool_t3":-2.0304,"late0":-0.0046,"late1":0.1249,"late2":0.0425,"odd_widen":-0.2474,"odd_turn_x0":-0.091,"odd_turn_x1":-0.1891,"odd_empty_x0":0.2051,"odd_empty_x1":-0.2995,"odd_quantize_x0":0.1294,"odd_quantize_x1":0.2566,"odd_place0":0.1929,"odd_place1":0.0622,"odd_empty_p0":0.3089,"odd_empty_p1":0.0933,"odd_embed0":-0.0626,"odd_embed1":0.1718,"odd_finish0":-0.1526,"odd_finish1":-0.0912,"odd_turn_h":0.0341,"odd_empty_h":0.4252,"odd_quantize_hx":-0.1274,"odd_feats":-0.0392,"odd_empty_f":-0.0168,"tail_embed0_14":-0.0609,"tail_embed0_15":0.0339,"tail_embed1_14":0.1319,"tail_embed1_15":0.1135,"tail_finish0_14":0.049,"tail_finish0_15":-0.104,"tail_finish1_14":-0.1521,"tail_finish1_15":0.0239,"tail_turn_h_14":0.2957,"tail_turn_h_15":0.0366,"tail_empty_h_14":-0.1201,"tail_empty_h_15":-0.3125,"tail_quantize_hx_14":-0.181,"tail_quantize_hx_15":0.0335,"tail_feats_14":0.177,"tail_feats_15":-0.0273,"tail_empty_f_14":0.2037,"tail_empty_f_15":0.0285,"lo00":-0.038,"lo01":1.1097,"lo10":0.1455,"lo11":1.2804}
-DQ = {"x0a":-4.512,"w00":-17.1473,"w10":-86.2143,"x0b":46.2804,"w20":-41.6917,"gain":24.0272,"pos":46.8802,"w01":24.0172,"w11":-42.0443,"w21":-72.8333,"scale":53.9738,"x":47.9936,"proj":55.8693,"pool":44.2499}
-ON_S = {"wi00":0,"wi10":0,"wi20":1,"wi01":0,"wi11":0,"wi21":1}
-H_ON_S = [0,1,1,0,1,1,1,0,1,0,1,1,0,0,0,1]
+QUARTER = 256
+SPLIT_TILES = 2
+BIG = 11
+ALIGN = 64
 
 
 def tile_tubelet_embed_pool_s8_kernel(
@@ -43,399 +39,397 @@ def tile_tubelet_embed_pool_s8_kernel(
         psum = ctx.enter_context(tc.psum_pool(name="psum", bufs=1))
         ctx.enter_context(tc.manual_schedule())
 
-        scale_bc = keep.tile([P, K], F32, align_bytes=64)
-        scale_k = keep.tile([P, KP, 4], F32)
-        nc.scalar.dma_start(out=scale_k[:], in_=x_scale.rearrange("o (c p t) -> p (o c) t", p=P, t=4))
-        gain_bf = keep.tile([P, 4, 4], BF16)
-
-        ident = keep.tile([P, P], F32, align_bytes=64)
+        ident = keep.tile([P, P], F32, align_bytes=ALIGN)
         make_identity(nc, ident[:])
-        pos = keep.tile([P, 4, N], BF16, align_bytes=64)
+        pos = keep.tile([P, 4, N], BF16, align_bytes=ALIGN)
         nc.gpsimd.memset(pos[64:128].rearrange("p t d -> p (t d)").bitcast(F32), 0.0)
-        proj_s = keep.tile([P, 2, R], U8, align_bytes=64)
-        nc.gpsimd.memset(proj_s[:].rearrange("p g n -> p (g n)").bitcast(I32), 0)
+        proj_s = keep.tile([P, 2, R], U8, align_bytes=ALIGN)
+        nc.gpsimd.memset(proj_s[:].rearrange("p b n -> p (b n)").bitcast(I32), 0)
 
-        x_rows = x_bytes.rearrange("(g p t) k -> g p t k", p=P, t=4)
-        xr = []
-        for s in range(TILES // 2):
-            xr.append(keep.tile([P, 2, K], U8, name="xr%d" % s, align_bytes=64))
-
-        def load_x(s, js):
-            g, t0 = s // 2, 2 * (s % 2)
-            nc.sync.dma_start(out=xr[s][:, js, :], in_=x_rows[g][:, t0 + js.start : t0 + js.stop, :])
-
-        w_rows = w.rearrange("(c p j) n -> c p j n", p=P, j=4)
-        w_raw = {}
-        for h in range(2):
-            for c in range(KP):
-                w_raw[c, h] = work.tile([P, 4, HALF], BF16, name="w_raw%d%d" % (c, h), tag="big", bufs=11, align_bytes=64)
-
-        def load_w(c, h):
-            nc.sync.dma_start(out=w_raw[c, h][:], in_=w_rows[c][:, :, h * HALF : (h + 1) * HALF])
-
-        proj_w = keep.tile([P, 2, 2 * R], U8, align_bytes=64)
-        pool_raw = keep.tile([P, 2, M], BF16, align_bytes=64)
-
-        def load_pos():
-            nc.sync.dma_start(out=pos[0:64], in_=space_pos.rearrange("(k t) d -> k t d", t=4))
-            nc.sync.dma_start(out=pos[64:72], in_=time_pos.unsqueeze(1).to_broadcast([T, 4, N]))
-
-        def load_scale():
-            nc.sync.dma_start(out=scale_bc[:], in_=x_scale.rearrange("o k -> (o k)").partition_broadcast(P))
-
-        def load_gain():
-            nc.sync.dma_start(out=gain_bf[:], in_=gain.rearrange("(g p t) -> p g t", p=P, t=4))
-
-        def load_proj():
-            for q in range(4):
-                nc.sync.dma_start(
-                    out=proj_s[32 * q : 32 * q + 4].bitcast(I32),
-                    in_=proj_scales[:, 4 * q : 4 * q + 4, :].rearrange("g q n -> q g n").bitcast(I32),
-                )
-            nc.sync.dma_start(out=proj_w[:].bitcast(I32), in_=proj_words.rearrange("g p c -> p g c").bitcast(I32))
-
-        def load_pool():
-            nc.sync.dma_start(out=pool_raw[:], in_=pool.rearrange("(a p) m -> p a m", p=P))
-
-        loads = [
-            (DQ["x0a"], load_x, (0, slice(0, 1))), (DQ["x0b"], load_x, (0, slice(1, 2))),
-            (DQ["pos"], load_pos, ()), (DQ["scale"], load_scale, ()), (DQ["gain"], load_gain, ()), (DQ["proj"], load_proj, ()), (DQ["pool"], load_pool, ()),
-        ]
-        for h in range(2):
-            for c in range(KP):
-                loads.append((DQ["w%d%d" % (c, h)], load_w, (c, h)))
-        for s in range(1, TILES // 2):
-            loads.append((DQ["x"] + s * 3, load_x, (s, slice(0, 2))))
-        for when, fn, args in sorted(loads, key=lambda x: x[0]):
-            fn(*args)
-
-        gain_f = keep.tile([P, TILES], F32, align_bytes=64)
-        sel = keep.tile([P, 4, 2, 64], BF16, align_bytes=64)
-        w_c = {}
-        w_s = {}
-        for h in range(2):
-            for c in range(KP):
-                w_c[c, h] = keep.tile([P, HALF], U32, name="w_c%d%d" % (c, h), align_bytes=64)
-                w_s[c, h] = keep.tile([P, HALF], U8, name="w_s%d%d" % (c, h), align_bytes=64)
-        h_c = []
-        h_s = []
-        for g in range(4):
-            h_c.append(keep.tile([P, N], U32, name="h_c%d" % g, align_bytes=64))
-            h_s.append(keep.tile([P, N], U8, name="h_s%d" % g, align_bytes=64))
-        p_c = keep.tile([P, 4, 2 * P], U32, align_bytes=64)
-        p_s = keep.tile([P, 4, 2 * P], U8, align_bytes=64)
-
-        xb = {}
-        xi = {}
-        xc = {}
-        xs = {}
-        pg = {}
-        hn = {}
-        hi = {}
-        hx = {}
-        hc = {}
-        hs = {}
-        wi = {}
-        ps_e = {}
-        px = {}
-        pp = {}
-        ph = {}
-        pf = {}
-
-        def widen(i):
-            xb_t = work.tile([P, K], BF16, bufs=3, align_bytes=64)
-            xb[i] = xb_t
-            codes = xr[i // 2][:, i % 2, :].bitcast(F8)
-            if i < EARLY:
-                nc.scalar.copy(out=xb_t[:], in_=codes)
-            else:
-                nc.vector.tensor_tensor(out=xb_t[:], in0=codes, in1=scale_bc[:], op=MULT)
-
-        banks = ((0, 2), (2, 1))
-
-        def turn_x(i, b):
-            words = xb[i][:].bitcast(F32)
-            c0, nk = banks[b]
-            if i not in xi:
-                xi_t = work.tile([P, KP, P, 2], F32, bufs=3, align_bytes=64)
-                xi[i] = xi_t
-            ps_x = psum.tile([P, nk, 2, P], F32, bufs=BX)
-            px[i, b] = ps_x
-            for c in range(nk):
-                for u in range(2):
-                    k0 = 256 * (c0 + c)
-                    nc.tensor.transpose(ps_x[:, c, u, :], words[:, k0 + u : k0 + 256 : 2], ident[:])
-
-        def empty_x(i, b):
-            c0, nk = banks[b]
-            if i >= EARLY:
-                nc.scalar.copy(out=xi[i][:, c0 : c0 + nk], in_=px[i, b][:].rearrange("p c u m -> p c m u"))
-                return
-            raw = px[i, b][:].rearrange("p c u m -> p (c u m)").bitcast(BF16)
-            raw = raw.rearrange("p (c u m e) -> p c m u e", c=nk, u=2, e=2)
-            dst = xi[i][:].rearrange("p c m u -> p (c m u)").bitcast(BF16)
-            dst = dst.rearrange("p (c m u e) -> p c m u e", c=KP, u=2, e=2)
-            for c in range(nk):
-                by = scale_k[:, c0 + c].rearrange("p (u e) -> p u e", u=2).unsqueeze(1).to_broadcast([P, P, 2, 2])
-                nc.vector.tensor_tensor(out=dst[:, c0 + c], in0=raw[:, c], in1=by, op=MULT)
-
-        def quantize_x(i, b):
-            if i not in xc:
-                xc_t = work.tile([P, KP, P], U32, bufs=3, align_bytes=64)
-                xs_t = work.tile([P, KP, P], U8, bufs=3, align_bytes=64)
-                xc[i] = xc_t
-                xs[i] = xs_t
-            cs = slice(banks[b][0], sum(banks[b]))
-            nc.vector.quantize_mx(
-                out=xc[i][:, cs].rearrange("p c m -> p (c m)").bitcast(F8X4),
-                scales=xs[i][:, cs].rearrange("p c m -> p (c m)"),
-                in_=xi[i][:, cs].rearrange("p c m u -> p (c m u)").bitcast(BF16),
+        select = keep.tile([P, GROUPS, 2, 64], BF16, align_bytes=ALIGN)
+        for g in range(GROUPS):
+            nc.vector.tensor_tensor(
+                out=select[:, g],
+                in0=ident[:, 0:64].unsqueeze(1).to_broadcast([P, 2, 64]),
+                in1=ident[:, 64 + 2 * g : 66 + 2 * g].unsqueeze(2).to_broadcast([P, 2, 64]),
+                op=ADD,
             )
 
-        def group_w(c, h, eng):
-            wi_t = work.tile([P, HALF, 4], BF16, bufs=3, align_bytes=64)
-            wi[c, h] = wi_t
-            src = w_raw[c, h][:].rearrange("p j (q u e) -> p q j u e", u=2, e=2)
-            dst = wi_t[:].rearrange("p (u q e) j -> p q j u e", u=2, e=2)
-            if eng == "s":
-                nc.scalar.copy(out=dst, in_=src)
-            else:
-                nc.vector.tensor_copy(out=dst, in_=src)
+        x_raw = []
+        for s in range(TILES // 2):
+            x_raw.append(keep.tile([P, 2, K], U8, name="x_raw%d" % s, align_bytes=ALIGN))
+        scale_rows = keep.tile([P, K], F32, align_bytes=ALIGN)
+        scale_k = keep.tile([P, PASSES, 4], F32)
+        gain_raw = keep.tile([P, GROUPS, 4], BF16)
+        gain_col = keep.tile([P, TILES], F32, align_bytes=ALIGN)
+        pool_raw = keep.tile([P, 2, M], BF16, align_bytes=ALIGN)
+        proj_w = keep.tile([P, 2, 2 * R], U8, align_bytes=ALIGN)
+        w_raw = {}
+        for h in range(2):
+            for c in range(PASSES):
+                w_raw[c, h] = work.tile(
+                    [P, 4, HALF], BF16, name="w_raw%d%d" % (c, h), tag="big", bufs=BIG, align_bytes=ALIGN
+                )
+
+        w_codes = {}
+        w_scales = {}
+        for h in range(2):
+            for c in range(PASSES):
+                w_codes[c, h] = keep.tile([P, HALF], U32, name="w_codes%d%d" % (c, h), align_bytes=ALIGN)
+                w_scales[c, h] = keep.tile([P, HALF], U8, name="w_scales%d%d" % (c, h), align_bytes=ALIGN)
+        h_codes = []
+        h_scales = []
+        for g in range(GROUPS):
+            h_codes.append(keep.tile([P, N], U32, name="h_codes%d" % g, align_bytes=ALIGN))
+            h_scales.append(keep.tile([P, N], U8, name="h_scales%d" % g, align_bytes=ALIGN))
+        p_codes = keep.tile([P, GROUPS, L], U32, align_bytes=ALIGN)
+        p_scales = keep.tile([P, GROUPS, L], U8, align_bytes=ALIGN)
+
+        def load_w(c, h):
+            rows = w.rearrange("(c p j) n -> c p j n", p=P, j=4)[c]
+            nc.sync.dma_start(out=w_raw[c, h][:], in_=rows[:, :, h * HALF : (h + 1) * HALF])
+
+        def load_x(first, count):
+            g, t = first // 4, first % 4
+            rows = x_bytes.rearrange("(g p t) k -> g p t k", p=P, t=4)[g]
+            slot = first % 2
+            nc.sync.dma_start(out=x_raw[first // 2][:, slot : slot + count, :], in_=rows[:, t : t + count, :])
+
+        nc.scalar.dma_start(out=scale_k[:], in_=x_scale.rearrange("o (c p t) -> p (o c) t", p=P, t=4))
+        load_w(2, 1)
+        load_w(1, 0)
+        load_w(2, 0)
+        load_w(1, 1)
+        nc.sync.dma_start(out=pool_raw[:], in_=pool.rearrange("(a p) m -> p a m", p=P))
+        load_w(0, 1)
+        nc.sync.dma_start(out=gain_raw[:], in_=gain.rearrange("(g p t) -> p g t", p=P, t=4))
+        load_x(0, 1)
+        load_w(0, 0)
+        load_x(1, 1)
+        nc.sync.dma_start(out=pos[0:64], in_=space_pos.rearrange("(k t) d -> k t d", t=4))
+        nc.sync.dma_start(out=pos[64:72], in_=time_pos.unsqueeze(1).to_broadcast([T, 4, N]))
+        nc.sync.dma_start(out=scale_rows[:], in_=x_scale.rearrange("o k -> (o k)").partition_broadcast(P))
+        for i in range(2, TILES, 2):
+            load_x(i, 2)
+        for q in range(4):
+            nc.sync.dma_start(
+                out=proj_s[32 * q : 32 * q + 4].bitcast(I32),
+                in_=proj_scales[:, 4 * q : 4 * q + 4, :].rearrange("b r n -> r b n").bitcast(I32),
+            )
+        nc.sync.dma_start(out=proj_w[:].bitcast(I32), in_=proj_words.rearrange("b p n -> p b n").bitcast(I32))
+
+        w_inter = {}
+        pool_ps = {}
+        pool_inter = {}
+        x_wide = {}
+        x_ps = {}
+        x_inter = {}
+        x_codes = {}
+        x_scales = {}
+        term_ps = {}
+        term = {}
+        e_ps = {}
+        h_rows = {}
+        h_ps = {}
+        hf_inter = {}
+        hf_codes = {}
+        hf_scales = {}
+        feats_ps = {}
+        ht_inter = {}
+        latents_ps = {}
+
+        def interleave_w(c, h, copy):
+            w_i = work.tile([P, HALF, 4], BF16, bufs=3, align_bytes=ALIGN)
+            w_inter[c, h] = w_i
+            copy(
+                out=w_i[:].rearrange("p (u q e) j -> p q j u e", u=2, e=2),
+                in_=w_raw[c, h][:].rearrange("p j (q u e) -> p q j u e", u=2, e=2),
+            )
 
         def quantize_w(c, h):
             nc.vector.quantize_mx(
-                out=w_c[c, h][:].bitcast(F8X4), scales=w_s[c, h][:], in_=wi[c, h][:].rearrange("p n j -> p (n j)")
+                out=w_codes[c, h][:].bitcast(F8X4),
+                scales=w_scales[c, h][:],
+                in_=w_inter[c, h][:].rearrange("p n j -> p (n j)"),
+            )
+
+        def turn_pool(g):
+            words = pool_raw[:].rearrange("p a m -> p (a m)").bitcast(F32)
+            turned = psum.tile([P, 2, 2, P], F32, bufs=2)
+            pool_ps[g] = turned
+            for a in range(2):
+                for u in range(2):
+                    m0 = a * (M // 2) + 256 * g
+                    nc.tensor.transpose(turned[:, a, u, :], words[:, m0 + u : m0 + 256 : 2], ident[:])
+
+        def empty_pool(g):
+            pool_i = work.tile([P, 2, P, 2], F32, bufs=4, align_bytes=ALIGN)
+            pool_inter[g] = pool_i
+            nc.scalar.copy(out=pool_i[:], in_=pool_ps[g][:].rearrange("p a u l -> p a l u"))
+
+        def quantize_pool(g):
+            nc.vector.quantize_mx(
+                out=p_codes[:, g].bitcast(F8X4),
+                scales=p_scales[:, g],
+                in_=pool_inter[g][:].rearrange("p a l u -> p (a l u)").bitcast(BF16),
+            )
+
+        x_banks = ((0, 2), (2, 1))
+
+        def widen_x(i):
+            wide = work.tile([P, K], BF16, bufs=3, align_bytes=ALIGN)
+            x_wide[i] = wide
+            values = x_raw[i // 2][:, i % 2, :].bitcast(F8)
+            if i < SPLIT_TILES:
+                nc.scalar.copy(out=wide[:], in_=values)
+            else:
+                nc.vector.tensor_tensor(out=wide[:], in0=values, in1=scale_rows[:], op=MULT)
+
+        def turn_x(i, b):
+            first, count = x_banks[b]
+            words = x_wide[i][:].bitcast(F32)
+            x_turned = psum.tile([P, count, 2, P], F32, bufs=2)
+            x_ps[i, b] = x_turned
+            for c in range(count):
+                for u in range(2):
+                    k0 = 256 * (first + c)
+                    nc.tensor.transpose(x_turned[:, c, u, :], words[:, k0 + u : k0 + 256 : 2], ident[:])
+
+        def empty_x(i, b):
+            first, count = x_banks[b]
+            if b == 0:
+                x_i = work.tile([P, PASSES, P, 2], F32, bufs=3, align_bytes=ALIGN)
+                x_inter[i] = x_i
+            if i >= SPLIT_TILES:
+                nc.scalar.copy(
+                    out=x_inter[i][:, first : first + count], in_=x_ps[i, b][:].rearrange("p c u m -> p c m u")
+                )
+                return
+            raw = x_ps[i, b][:].rearrange("p c u m -> p (c u m)").bitcast(BF16)
+            raw = raw.rearrange("p (c u m e) -> p c m u e", c=count, u=2, e=2)
+            dst = x_inter[i][:].rearrange("p c m u -> p (c m u)").bitcast(BF16)
+            dst = dst.rearrange("p (c m u e) -> p c m u e", c=PASSES, u=2, e=2)
+            for c in range(count):
+                scale = scale_k[:, first + c].rearrange("p (u e) -> p u e", u=2)
+                scale = scale.unsqueeze(1).to_broadcast([P, P, 2, 2])
+                nc.vector.tensor_tensor(out=dst[:, first + c], in0=raw[:, c], in1=scale, op=MULT)
+
+        def quantize_x(i, b):
+            first, count = x_banks[b]
+            if b == 0:
+                codes = work.tile([P, PASSES, P], U32, bufs=3, align_bytes=ALIGN)
+                scales = work.tile([P, PASSES, P], U8, bufs=3, align_bytes=ALIGN)
+                x_codes[i] = codes
+                x_scales[i] = scales
+            cs = slice(first, first + count)
+            nc.vector.quantize_mx(
+                out=x_codes[i][:, cs].rearrange("p c m -> p (c m)").bitcast(F8X4),
+                scales=x_scales[i][:, cs].rearrange("p c m -> p (c m)"),
+                in_=x_inter[i][:, cs].rearrange("p c m u -> p (c m u)").bitcast(BF16),
             )
 
         def place(i, h):
-            g, t = i // 4, i % 4
-            if i not in pg:
-                pg_t = work.tile([P, 2, HALF], F32, tag="big", bufs=11, align_bytes=64)
-                pg[i] = pg_t
-            ps_p = psum.tile([P, HALF], F32, bufs=BP)
-            pp[i, h] = ps_p
+            placed = psum.tile([P, HALF], F32, bufs=1)
+            term_ps[i, h] = placed
             nc.tensor.matmul(
-                out=ps_p[:],
-                lhsT=sel[:, g].rearrange("p a b -> p (a b)"),
-                rhs=pos[:, t, h * HALF : (h + 1) * HALF],
+                out=placed[:],
+                lhsT=select[:, i // 4].rearrange("p a b -> p (a b)"),
+                rhs=pos[:, i % 4, h * HALF : (h + 1) * HALF],
                 start=True,
                 stop=True,
             )
 
-        def empty_p(i, h):
+        def scale_term(i, h):
+            if h == 0:
+                term_i = work.tile([P, 2, HALF], F32, tag="big", bufs=BIG, align_bytes=ALIGN)
+                term[i] = term_i
             nc.scalar.activation(
-                out=pg[i][:, h].rearrange("p (u q e) -> p u q e", u=2, e=2),
-                in_=pp[i, h][:].rearrange("p (q u e) -> p u q e", u=2, e=2),
+                out=term[i][:, h].rearrange("p (u q e) -> p u q e", u=2, e=2),
+                in_=term_ps[i, h][:].rearrange("p (q u e) -> p u q e", u=2, e=2),
                 func=COPY,
-                scale=gain_f[:, i : i + 1],
+                scale=gain_col[:, i : i + 1],
             )
 
         def embed(i, h):
-            acc = psum.tile([P, HALF], F32, bufs=BE)
-            ps_e[i, h] = acc
-            for c in range(KP):
+            acc = psum.tile([P, HALF], F32, bufs=2)
+            e_ps[i, h] = acc
+            for c in range(PASSES):
                 nc.tensor.matmul_mx(
                     out=acc[:],
-                    lhsT=xc[i][:, c].bitcast(F8X4),
-                    lhsT_scale=xs[i][:, c],
-                    rhs=w_c[c, h][:].bitcast(F8X4),
-                    rhs_scale=w_s[c, h][:],
+                    lhsT=x_codes[i][:, c].bitcast(F8X4),
+                    lhsT_scale=x_scales[i][:, c],
+                    rhs=w_codes[c, h][:].bitcast(F8X4),
+                    rhs_scale=w_scales[c, h][:],
                     start=(c == 0),
-                    stop=(c == KP - 1),
+                    stop=(c == PASSES - 1),
                 )
 
         def finish_h(i, h):
             g, t = i // 4, i % 4
-            if g not in hn:
-                hn_t = work.tile([P, 4, N], BF16, bufs=2, align_bytes=64)
-                hn[g] = hn_t
+            if t == 0 and h == 0:
+                rows = work.tile([P, 4, N], BF16, bufs=2, align_bytes=ALIGN)
+                h_rows[g] = rows
             nc.vector.scalar_tensor_tensor(
-                out=hn[g][:, t, h * HALF : (h + 1) * HALF],
-                in0=ps_e[i, h][:],
-                scalar=gain_f[:, i : i + 1],
-                in1=pg[i][:, h],
+                out=h_rows[g][:, t, h * HALF : (h + 1) * HALF],
+                in0=e_ps[i, h][:],
+                scalar=gain_col[:, i : i + 1],
+                in1=term[i][:, h],
                 op0=MULT,
                 op1=ADD,
             )
 
         def turn_h(i):
             g, t = i // 4, i % 4
-            words = hn[g][:].rearrange("p t d -> p (t d)").bitcast(F32)
-            ps_h = psum.tile([P, 2, 2, P], F32, bufs=BH)
+            words = h_rows[g][:].rearrange("p t d -> p (t d)").bitcast(F32)
+            turned = psum.tile([P, 2, 2, P], F32, bufs=2)
+            h_ps[i] = turned
             for b in range(2):
                 for u in range(2):
                     d0 = t * HALF + 256 * b + 128 * u
-                    nc.tensor.transpose(ps_h[:, b, u, :], words[:, d0 : d0 + 128], ident[:])
-            ph[i] = ps_h
+                    nc.tensor.transpose(turned[:, b, u, :], words[:, d0 : d0 + 128], ident[:])
 
         def empty_h(i):
-            hx_t = work.tile([P, 2, P, 2], F32, bufs=3, align_bytes=64)
-            hx[i] = hx_t
-            nc.scalar.copy(out=hx_t[:], in_=ph[i][:].rearrange("p b u m -> p b m u"))
+            hf_i = work.tile([P, 2, P, 2], F32, bufs=3, align_bytes=ALIGN)
+            hf_inter[i] = hf_i
+            nc.scalar.copy(out=hf_i[:], in_=h_ps[i][:].rearrange("p b u m -> p b m u"))
 
-        def quantize_hx(i):
-            hc_t = work.tile([P, 2, P], U32, bufs=2, align_bytes=64)
-            hs_t = work.tile([P, 2, P], U8, bufs=2, align_bytes=64)
-            hc[i] = hc_t
-            hs[i] = hs_t
+        def quantize_features(i):
+            codes_f = work.tile([P, 2, P], U32, bufs=2, align_bytes=ALIGN)
+            scales_f = work.tile([P, 2, P], U8, bufs=2, align_bytes=ALIGN)
+            hf_codes[i] = codes_f
+            hf_scales[i] = scales_f
             nc.vector.quantize_mx(
-                out=hc_t[:].rearrange("p b m -> p (b m)").bitcast(F8X4),
-                scales=hs_t[:].rearrange("p b m -> p (b m)"),
-                in_=hx[i][:].rearrange("p b m u -> p (b m u)").bitcast(BF16),
+                out=codes_f[:].rearrange("p b m -> p (b m)").bitcast(F8X4),
+                scales=scales_f[:].rearrange("p b m -> p (b m)"),
+                in_=hf_inter[i][:].rearrange("p b m u -> p (b m u)").bitcast(BF16),
             )
 
-        def feats(i):
-            g, t = i // 4, i % 4
-            ps_f = psum.tile([P, R], F32, bufs=BF)
+        def project(i):
+            projected = psum.tile([P, R], F32, bufs=1)
+            feats_ps[i] = projected
             for b in range(2):
                 nc.tensor.matmul_mx(
-                    out=ps_f[:],
-                    lhsT=hc[i][:, b].bitcast(F8X4),
-                    lhsT_scale=hs[i][:, b],
+                    out=projected[:],
+                    lhsT=hf_codes[i][:, b].bitcast(F8X4),
+                    lhsT_scale=hf_scales[i][:, b],
                     rhs=proj_w[:, b].bitcast(F4X4),
                     rhs_scale=proj_s[:, b],
                     start=(b == 0),
                     stop=(b == 1),
                 )
-            pf[i] = ps_f
 
-        def empty_f(i):
-            g, t = i // 4, i % 4
-            fo = work.tile([P, R], F32, bufs=3, align_bytes=64)
-            nc.scalar.copy(out=fo[:], in_=pf[i][:])
-            nc.sync.dma_start(out=out_0.rearrange("(g p t) r -> g t p r", p=P, t=4)[g, t], in_=fo[:])
+        def store_features(i):
+            feats = work.tile([P, R], F32, bufs=3, align_bytes=ALIGN)
+            nc.scalar.copy(out=feats[:], in_=feats_ps[i][:])
+            nc.sync.dma_start(out=out_0.rearrange("(g p t) r -> g t p r", p=P, t=4)[i // 4, i % 4], in_=feats[:])
 
-        def group_h(g, c, eng):
-            hi_t = work.tile([P, CH, 4], BF16, bufs=3, align_bytes=64)
-            hi[g, c] = hi_t
-            src = hn[g][:, :, c * CH : (c + 1) * CH].rearrange("p t (n i) -> p n t i", i=4)
-            dst = hi_t[:].rearrange("p (n i) t -> p n t i", i=4)
-            if eng == "s":
-                nc.scalar.copy(out=dst, in_=src)
-            else:
-                nc.vector.tensor_copy(out=dst, in_=src)
-
-        def quantize_h(g, c):
-            ds = slice(c * CH, (c + 1) * CH)
-            nc.vector.quantize_mx(
-                out=h_c[g][:, ds].bitcast(F8X4), scales=h_s[g][:, ds], in_=hi[g, c][:].rearrange("p d t -> p (d t)")
+        def interleave_h(n):
+            g, d0 = n // 4, QUARTER * (n % 4)
+            ht_i = work.tile([P, QUARTER, 4], BF16, bufs=3, align_bytes=ALIGN)
+            ht_inter[n] = ht_i
+            on_scalar = n % 3 != 1 and g < GROUPS - 1
+            copy = nc.scalar.copy if on_scalar else nc.vector.tensor_copy
+            copy(
+                out=ht_i[:].rearrange("p (n i) t -> p n t i", i=4),
+                in_=h_rows[g][:, :, d0 : d0 + QUARTER].rearrange("p t (n i) -> p n t i", i=4),
             )
 
-        pi = {}
+        def quantize_tokens(n):
+            g, d0 = n // 4, QUARTER * (n % 4)
+            nc.vector.quantize_mx(
+                out=h_codes[g][:, d0 : d0 + QUARTER].bitcast(F8X4),
+                scales=h_scales[g][:, d0 : d0 + QUARTER],
+                in_=ht_inter[n][:].rearrange("p d t -> p (d t)"),
+            )
 
-        def turn_pool(g):
-            words = pool_raw[:].rearrange("p a m -> p (a m)").bitcast(F32)
-            ps_h = psum.tile([P, 2, 2, P], F32, bufs=BH)
+        def pool_pass(g, h):
             for a in range(2):
-                for u in range(2):
-                    m0 = a * (M // 2) + 256 * g
-                    nc.tensor.transpose(ps_h[:, a, u, :], words[:, m0 + u : m0 + 256 : 2], ident[:])
-            ph["pool", g] = ps_h
+                nc.tensor.matmul_mx(
+                    out=latents_ps[a, h][:],
+                    lhsT=p_codes[:, g, a * P : (a + 1) * P].bitcast(F8X4),
+                    lhsT_scale=p_scales[:, g, a * P : (a + 1) * P],
+                    rhs=h_codes[g][:, h * HALF : (h + 1) * HALF].bitcast(F8X4),
+                    rhs_scale=h_scales[g][:, h * HALF : (h + 1) * HALF],
+                    start=(g == 0),
+                    stop=(g == GROUPS - 1),
+                )
 
-        def empty_pool(g):
-            pi_t = work.tile([P, 2, P, 2], F32, bufs=4, align_bytes=64)
-            pi[g] = pi_t
-            nc.scalar.copy(out=pi_t[:], in_=ph["pool", g][:].rearrange("p a u l -> p a l u"))
-
-        def quantize_pool(g):
-            nc.vector.quantize_mx(
-                out=p_c[:, g].bitcast(F8X4),
-                scales=p_s[:, g],
-                in_=pi[g][:].rearrange("p a l u -> p (a l u)").bitcast(BF16),
+        def store_latents(a, h):
+            lat = work.tile([P, HALF], F32, bufs=4, align_bytes=ALIGN)
+            copy = nc.vector.tensor_copy if a == 0 else nc.scalar.copy
+            copy(
+                out=lat[:].rearrange("p (q u e) -> p q u e", u=2, e=2),
+                in_=latents_ps[a, h][:].rearrange("p (u q e) -> p q u e", u=2, e=2),
             )
+            nc.sync.dma_start(out=out_1[a * P : (a + 1) * P, h * HALF : (h + 1) * HALF], in_=lat[:])
 
-        def cast_gain():
-            nc.vector.tensor_copy(out=gain_f[:], in_=gain_bf[:].rearrange("p g t -> p (g t)"))
+        scalar, vector = nc.scalar.copy, nc.vector.tensor_copy
+        interleave_w(1, 0, vector)
+        interleave_w(2, 1, scalar)
+        quantize_w(1, 0)
+        interleave_w(2, 0, scalar)
+        interleave_w(1, 1, vector)
+        quantize_w(1, 1)
+        turn_pool(0)
+        quantize_w(2, 1)
+        empty_pool(0)
+        quantize_w(2, 0)
+        turn_pool(1)
+        interleave_w(0, 1, vector)
+        quantize_pool(0)
+        nc.vector.tensor_copy(out=gain_col[:], in_=gain_raw[:].rearrange("p g t -> p (g t)"))
+        empty_pool(1)
+        interleave_w(0, 0, vector)
+        turn_pool(2)
+        turn_pool(3)
+        empty_pool(2)
+        quantize_pool(1)
+        quantize_w(0, 1)
+        quantize_w(0, 0)
+        widen_x(0)
+        empty_pool(3)
 
-        for g in range(4):
-            nc.vector.tensor_tensor(
-                out=sel[:, g],
-                in0=ident[:, 0:64].unsqueeze(1).to_broadcast([P, 2, 64]),
-                in1=ident[:, 64 + 2 * g : 66 + 2 * g].unsqueeze(2).to_broadcast([P, 2, 64]),
-                op=ADD,
-            )
-        acc = {}
-
-        def pool_pass(g, a, h):
-            if (a, h) not in acc:
-                if a == 0:
-                    ps_x = psum.tile([P, HALF], F32, bufs=BX)
-                    acc[a, h] = ps_x
-                elif h == 0:
-                    ps_p = psum.tile([P, HALF], F32, bufs=BP)
-                    acc[a, h] = ps_p
-                else:
-                    ps_l = psum.tile([P, HALF], F32, tag="acc", bufs=BE)
-                    acc[a, h] = ps_l
-            nc.tensor.matmul_mx(
-                out=acc[a, h][:],
-                lhsT=p_c[:, g, a * P : (a + 1) * P].bitcast(F8X4),
-                lhsT_scale=p_s[:, g, a * P : (a + 1) * P],
-                rhs=h_c[g][:, h * HALF : (h + 1) * HALF].bitcast(F8X4),
-                rhs_scale=h_s[g][:, h * HALF : (h + 1) * HALF],
-                start=(g == 0),
-                stop=(g == 3),
-            )
-
-        def latents_out(a, h):
-            lo = work.tile([P, HALF], F32, bufs=4, align_bytes=64)
-            src = acc[a, h][:].rearrange("p (u q e) -> p q u e", u=2, e=2)
-            dst = lo[:].rearrange("p (q u e) -> p q u e", u=2, e=2)
-            if a == 0:
-                nc.vector.tensor_copy(out=dst, in_=src)
-            else:
-                nc.scalar.copy(out=dst, in_=src)
-            nc.sync.dma_start(out=out_1[a * P : (a + 1) * P, h * HALF : (h + 1) * HALF], in_=lo[:])
-
-        plan = []
-
-        def at(when, fn, *args):
-            plan.append((when, len(plan), fn, args))
-
-        for i in range(TILES):
-
-            def stage(key, fn, *args, rate=1.0, late=0):
-                if i >= 14 and key in TAIL:
-                    late = late + AT["tail_%s_%d" % (key, i)]
-                at(i * rate + late + AT[key] + (i % 2) * AT["odd_" + key], fn, *args)
-
-            stage("widen", widen, i)
-            early = AT["late%d" % i] if i < 3 else 0
-            for h in range(2):
-                stage("turn_x%d" % h, turn_x, i, h)
-                stage("empty_x%d" % h, empty_x, i, h)
-                stage("quantize_x%d" % h, quantize_x, i, h)
-                stage("place%d" % h, place, i, h, rate=AT["place_rate"])
-                stage("empty_p%d" % h, empty_p, i, h, rate=AT["place_rate"])
-                stage("embed%d" % h, embed, i, h, late=h * early)
-                stage("finish%d" % h, finish_h, i, h, late=h * early)
-            stage("turn_h", turn_h, i, late=early)
-            stage("empty_h", empty_h, i, late=early)
-            stage("quantize_hx", quantize_hx, i)
-            stage("feats", feats, i)
-            stage("empty_f", empty_f, i)
-        at(AT["gain"], cast_gain)
-        for g in range(4):
-            at(AT["pool_t%d" % g], turn_pool, g)
-            at(AT["pool_t%d" % g] + AT["pool_e"], empty_pool, g)
-            at(AT["pool_t%d" % g] + AT["pool_q"], quantize_pool, g)
-            for c in range(4):
-                e = "s" if H_ON_S[4 * g + c] else "v"
-                if g < 3:
-                    at(4 * g + c * AT["group_step"] + AT["group_h"], group_h, g, c, e)
-                    at(4 * g + c * AT["group_step"] + AT["quantize_h"], quantize_h, g, c)
-                else:
-                    at(AT["last_g%d" % c], group_h, g, c, e)
-                    at(AT["last_q%d" % c], quantize_h, g, c)
-        for h in range(2):
-            for c in range(KP):
-                e = "s" if ON_S["wi%d%d" % (c, h)] else "v"
-                at(AT["wi%d%d" % (c, h)], group_w, c, h, e)
-                at(AT["wq%d%d" % (c, h)], quantize_w, c, h)
+        steps = (
+            (turn_x, 1, (0,)),
+            (widen_x, 2, ()),
+            (store_features, -3, ()),
+            (empty_x, 1, (0,)),
+            (turn_x, 1, (1,)),
+            (turn_h, -1, ()),
+            (place, 1, (0,)),
+            (embed, 0, (0,)),
+            (scale_term, 1, (0,)),
+            (embed, 0, (1,)),
+            (empty_x, 1, (1,)),
+            (interleave_h, -4, ()),
+            (quantize_features, -2, ()),
+            (place, 1, (1,)),
+            (scale_term, 1, (1,)),
+            (quantize_tokens, -5, ()),
+            (empty_h, -1, ()),
+            (finish_h, 0, (0,)),
+            (project, -2, ()),
+            (finish_h, 0, (1,)),
+            (quantize_x, 1, (0,)),
+            (quantize_x, 1, (1,)),
+        )
+        for i in range(-1, TILES + 5):
+            if i in (2, 3):
+                quantize_pool(i)
+            if i == TILES:
+                banks = (("x_turned", 2), ("x_turned", 2), ("placed", 1), ("acc", 2))
+                for n, (tag, bufs) in enumerate(banks):
+                    bank = psum.tile([P, HALF], F32, tag=tag, bufs=bufs)
+                    latents_ps[n // 2, n % 2] = bank
+            if TILES <= i < TILES + 3:
+                for h in range(2):
+                    pool_pass(i - TILES, h)
+            for stage, ahead, part in steps:
+                if 0 <= i + ahead < TILES:
+                    stage(i + ahead, *part)
+            if i == TILES + 2:
+                pool_pass(3, 0)
+        pool_pass(3, 1)
         for h in range(2):
             for a in range(2):
-                for g in range(4):
-                    at(AT["lat%d" % g] if g < 3 else AT["lat3%d" % h], pool_pass, g, a, h)
-                at(30 + AT["lo%d%d" % (a, h)], latents_out, a, h)
-        for when, n, fn, args in sorted(plan, key=lambda x: (x[0], x[1])):
-            fn(*args)
+                store_latents(a, h)

from contextlib import ExitStack

import concourse.mybir as mybir
from concourse.masks import make_identity

M, T, K, N, R, L = 2048, 8, 1536, 1024, 512, 256
FLOPS = 2 * (M * K * N + M * N * R + L * M * N)

F32 = mybir.dt.float32
BF16 = mybir.dt.bfloat16
I32 = mybir.dt.int32
U32 = mybir.dt.uint32
U8 = mybir.dt.uint8
F8 = mybir.dt.float8_e4m3fn
F8X4 = mybir.dt.float8_e4m3fn_x4
F4X4 = mybir.dt.float4_e2m1fn_x4
COPY = mybir.ActivationFunctionType.Copy
ADD = mybir.AluOpType.add
MULT = mybir.AluOpType.mult

P = 128
PASSES = K // 512
GROUPS = M // 512
TILES = M // P
HALF = 512
QUARTER = 256
SPLIT_TILES = 2
BIG = 11
ALIGN = 64


def tile_tubelet_embed_pool_s8_kernel(
    tc, x_bytes, x_scale, w, time_pos, space_pos, gain, proj_words, proj_scales, pool, out_0, out_1
):
    nc = tc.nc
    with ExitStack() as ctx:
        keep = ctx.enter_context(tc.tile_pool(name="keep", bufs=1))
        work = ctx.enter_context(tc.tile_pool(name="work", bufs=2))
        psum = ctx.enter_context(tc.psum_pool(name="psum", bufs=1))
        ctx.enter_context(tc.manual_schedule())

        ident = keep.tile([P, P], F32, align_bytes=ALIGN)
        make_identity(nc, ident[:])
        pos = keep.tile([P, 4, N], BF16, align_bytes=ALIGN)
        nc.gpsimd.memset(pos[64:128].rearrange("p t d -> p (t d)").bitcast(F32), 0.0)
        proj_s = keep.tile([P, 2, R], U8, align_bytes=ALIGN)
        nc.gpsimd.memset(proj_s[:].rearrange("p b n -> p (b n)").bitcast(I32), 0)

        select = keep.tile([P, GROUPS, 2, 64], BF16, align_bytes=ALIGN)
        for g in range(GROUPS):
            nc.vector.tensor_tensor(
                out=select[:, g],
                in0=ident[:, 0:64].unsqueeze(1).to_broadcast([P, 2, 64]),
                in1=ident[:, 64 + 2 * g : 66 + 2 * g].unsqueeze(2).to_broadcast([P, 2, 64]),
                op=ADD,
            )

        x_raw = []
        for s in range(TILES // 2):
            x_raw.append(keep.tile([P, 2, K], U8, name="x_raw%d" % s, align_bytes=ALIGN))
        scale_rows = keep.tile([P, K], F32, align_bytes=ALIGN)
        scale_k = keep.tile([P, PASSES, 4], F32)
        gain_raw = keep.tile([P, GROUPS, 4], BF16)
        gain_col = keep.tile([P, TILES], F32, align_bytes=ALIGN)
        pool_raw = keep.tile([P, 2, M], BF16, align_bytes=ALIGN)
        proj_w = keep.tile([P, 2, 2 * R], U8, align_bytes=ALIGN)
        w_raw = {}
        for h in range(2):
            for c in range(PASSES):
                w_raw[c, h] = work.tile(
                    [P, 4, HALF], BF16, name="w_raw%d%d" % (c, h), tag="big", bufs=BIG, align_bytes=ALIGN
                )

        w_codes = {}
        w_scales = {}
        for h in range(2):
            for c in range(PASSES):
                w_codes[c, h] = keep.tile([P, HALF], U32, name="w_codes%d%d" % (c, h), align_bytes=ALIGN)
                w_scales[c, h] = keep.tile([P, HALF], U8, name="w_scales%d%d" % (c, h), align_bytes=ALIGN)
        h_codes = []
        h_scales = []
        for g in range(GROUPS):
            h_codes.append(keep.tile([P, N], U32, name="h_codes%d" % g, align_bytes=ALIGN))
            h_scales.append(keep.tile([P, N], U8, name="h_scales%d" % g, align_bytes=ALIGN))
        p_codes = keep.tile([P, GROUPS, L], U32, align_bytes=ALIGN)
        p_scales = keep.tile([P, GROUPS, L], U8, align_bytes=ALIGN)

        def load_w(c, h):
            rows = w.rearrange("(c p j) n -> c p j n", p=P, j=4)[c]
            nc.sync.dma_start(out=w_raw[c, h][:], in_=rows[:, :, h * HALF : (h + 1) * HALF])

        def load_x(first, count):
            g, t = first // 4, first % 4
            rows = x_bytes.rearrange("(g p t) k -> g p t k", p=P, t=4)[g]
            slot = first % 2
            nc.sync.dma_start(out=x_raw[first // 2][:, slot : slot + count, :], in_=rows[:, t : t + count, :])

        nc.scalar.dma_start(out=scale_k[:], in_=x_scale.rearrange("o (c p t) -> p (o c) t", p=P, t=4))
        load_w(2, 1)
        load_w(1, 0)
        load_w(2, 0)
        load_w(1, 1)
        nc.sync.dma_start(out=pool_raw[:], in_=pool.rearrange("(a p) m -> p a m", p=P))
        load_w(0, 1)
        nc.sync.dma_start(out=gain_raw[:], in_=gain.rearrange("(g p t) -> p g t", p=P, t=4))
        load_x(0, 1)
        load_w(0, 0)
        load_x(1, 1)
        nc.sync.dma_start(out=pos[0:64], in_=space_pos.rearrange("(k t) d -> k t d", t=4))
        nc.sync.dma_start(out=pos[64:72], in_=time_pos.unsqueeze(1).to_broadcast([T, 4, N]))
        nc.sync.dma_start(out=scale_rows[:], in_=x_scale.rearrange("o k -> (o k)").partition_broadcast(P))
        for i in range(2, TILES, 2):
            load_x(i, 2)
        for q in range(4):
            nc.sync.dma_start(
                out=proj_s[32 * q : 32 * q + 4].bitcast(I32),
                in_=proj_scales[:, 4 * q : 4 * q + 4, :].rearrange("b r n -> r b n").bitcast(I32),
            )
        nc.sync.dma_start(out=proj_w[:].bitcast(I32), in_=proj_words.rearrange("b p n -> p b n").bitcast(I32))

        w_inter = {}
        pool_ps = {}
        pool_inter = {}
        x_wide = {}
        x_ps = {}
        x_inter = {}
        x_codes = {}
        x_scales = {}
        term_ps = {}
        term = {}
        e_ps = {}
        h_rows = {}
        h_ps = {}
        hf_inter = {}
        hf_codes = {}
        hf_scales = {}
        feats_ps = {}
        ht_inter = {}
        latents_ps = {}

        def interleave_w(c, h, copy):
            w_i = work.tile([P, HALF, 4], BF16, bufs=3, align_bytes=ALIGN)
            w_inter[c, h] = w_i
            copy(
                out=w_i[:].rearrange("p (u q e) j -> p q j u e", u=2, e=2),
                in_=w_raw[c, h][:].rearrange("p j (q u e) -> p q j u e", u=2, e=2),
            )

        def quantize_w(c, h):
            nc.vector.quantize_mx(
                out=w_codes[c, h][:].bitcast(F8X4),
                scales=w_scales[c, h][:],
                in_=w_inter[c, h][:].rearrange("p n j -> p (n j)"),
            )

        def turn_pool(g):
            words = pool_raw[:].rearrange("p a m -> p (a m)").bitcast(F32)
            turned = psum.tile([P, 2, 2, P], F32, bufs=2)
            pool_ps[g] = turned
            for a in range(2):
                for u in range(2):
                    m0 = a * (M // 2) + 256 * g
                    nc.tensor.transpose(turned[:, a, u, :], words[:, m0 + u : m0 + 256 : 2], ident[:])

        def empty_pool(g):
            pool_i = work.tile([P, 2, P, 2], F32, bufs=4, align_bytes=ALIGN)
            pool_inter[g] = pool_i
            nc.scalar.copy(out=pool_i[:], in_=pool_ps[g][:].rearrange("p a u l -> p a l u"))

        def quantize_pool(g):
            nc.vector.quantize_mx(
                out=p_codes[:, g].bitcast(F8X4),
                scales=p_scales[:, g],
                in_=pool_inter[g][:].rearrange("p a l u -> p (a l u)").bitcast(BF16),
            )

        x_banks = ((0, 2), (2, 1))

        def widen_x(i):
            wide = work.tile([P, K], BF16, bufs=3, align_bytes=ALIGN)
            x_wide[i] = wide
            values = x_raw[i // 2][:, i % 2, :].bitcast(F8)
            if i < SPLIT_TILES:
                nc.scalar.copy(out=wide[:], in_=values)
            else:
                nc.vector.tensor_tensor(out=wide[:], in0=values, in1=scale_rows[:], op=MULT)

        def turn_x(i, b):
            first, count = x_banks[b]
            words = x_wide[i][:].bitcast(F32)
            x_turned = psum.tile([P, count, 2, P], F32, bufs=2)
            x_ps[i, b] = x_turned
            for c in range(count):
                for u in range(2):
                    k0 = 256 * (first + c)
                    nc.tensor.transpose(x_turned[:, c, u, :], words[:, k0 + u : k0 + 256 : 2], ident[:])

        def empty_x(i, b):
            first, count = x_banks[b]
            if b == 0:
                x_i = work.tile([P, PASSES, P, 2], F32, bufs=3, align_bytes=ALIGN)
                x_inter[i] = x_i
            if i >= SPLIT_TILES:
                nc.scalar.copy(
                    out=x_inter[i][:, first : first + count], in_=x_ps[i, b][:].rearrange("p c u m -> p c m u")
                )
                return
            raw = x_ps[i, b][:].rearrange("p c u m -> p (c u m)").bitcast(BF16)
            raw = raw.rearrange("p (c u m e) -> p c m u e", c=count, u=2, e=2)
            dst = x_inter[i][:].rearrange("p c m u -> p (c m u)").bitcast(BF16)
            dst = dst.rearrange("p (c m u e) -> p c m u e", c=PASSES, u=2, e=2)
            for c in range(count):
                scale = scale_k[:, first + c].rearrange("p (u e) -> p u e", u=2)
                scale = scale.unsqueeze(1).to_broadcast([P, P, 2, 2])
                nc.vector.tensor_tensor(out=dst[:, first + c], in0=raw[:, c], in1=scale, op=MULT)

        def quantize_x(i, b):
            first, count = x_banks[b]
            if b == 0:
                codes = work.tile([P, PASSES, P], U32, bufs=3, align_bytes=ALIGN)
                scales = work.tile([P, PASSES, P], U8, bufs=3, align_bytes=ALIGN)
                x_codes[i] = codes
                x_scales[i] = scales
            cs = slice(first, first + count)
            nc.vector.quantize_mx(
                out=x_codes[i][:, cs].rearrange("p c m -> p (c m)").bitcast(F8X4),
                scales=x_scales[i][:, cs].rearrange("p c m -> p (c m)"),
                in_=x_inter[i][:, cs].rearrange("p c m u -> p (c m u)").bitcast(BF16),
            )

        def place(i, h):
            placed = psum.tile([P, HALF], F32, bufs=1)
            term_ps[i, h] = placed
            nc.tensor.matmul(
                out=placed[:],
                lhsT=select[:, i // 4].rearrange("p a b -> p (a b)"),
                rhs=pos[:, i % 4, h * HALF : (h + 1) * HALF],
                start=True,
                stop=True,
            )

        def scale_term(i, h):
            if h == 0:
                term_i = work.tile([P, 2, HALF], F32, tag="big", bufs=BIG, align_bytes=ALIGN)
                term[i] = term_i
            nc.scalar.activation(
                out=term[i][:, h].rearrange("p (u q e) -> p u q e", u=2, e=2),
                in_=term_ps[i, h][:].rearrange("p (q u e) -> p u q e", u=2, e=2),
                func=COPY,
                scale=gain_col[:, i : i + 1],
            )

        def embed(i, h):
            acc = psum.tile([P, HALF], F32, bufs=2)
            e_ps[i, h] = acc
            for c in range(PASSES):
                nc.tensor.matmul_mx(
                    out=acc[:],
                    lhsT=x_codes[i][:, c].bitcast(F8X4),
                    lhsT_scale=x_scales[i][:, c],
                    rhs=w_codes[c, h][:].bitcast(F8X4),
                    rhs_scale=w_scales[c, h][:],
                    start=(c == 0),
                    stop=(c == PASSES - 1),
                )

        def finish_h(i, h):
            g, t = i // 4, i % 4
            if t == 0 and h == 0:
                rows = work.tile([P, 4, N], BF16, bufs=2, align_bytes=ALIGN)
                h_rows[g] = rows
            nc.vector.scalar_tensor_tensor(
                out=h_rows[g][:, t, h * HALF : (h + 1) * HALF],
                in0=e_ps[i, h][:],
                scalar=gain_col[:, i : i + 1],
                in1=term[i][:, h],
                op0=MULT,
                op1=ADD,
            )

        def turn_h(i):
            g, t = i // 4, i % 4
            words = h_rows[g][:].rearrange("p t d -> p (t d)").bitcast(F32)
            turned = psum.tile([P, 2, 2, P], F32, bufs=2)
            h_ps[i] = turned
            for b in range(2):
                for u in range(2):
                    d0 = t * HALF + 256 * b + 128 * u
                    nc.tensor.transpose(turned[:, b, u, :], words[:, d0 : d0 + 128], ident[:])

        def empty_h(i):
            hf_i = work.tile([P, 2, P, 2], F32, bufs=3, align_bytes=ALIGN)
            hf_inter[i] = hf_i
            nc.scalar.copy(out=hf_i[:], in_=h_ps[i][:].rearrange("p b u m -> p b m u"))

        def quantize_features(i):
            codes_f = work.tile([P, 2, P], U32, bufs=2, align_bytes=ALIGN)
            scales_f = work.tile([P, 2, P], U8, bufs=2, align_bytes=ALIGN)
            hf_codes[i] = codes_f
            hf_scales[i] = scales_f
            nc.vector.quantize_mx(
                out=codes_f[:].rearrange("p b m -> p (b m)").bitcast(F8X4),
                scales=scales_f[:].rearrange("p b m -> p (b m)"),
                in_=hf_inter[i][:].rearrange("p b m u -> p (b m u)").bitcast(BF16),
            )

        def project(i):
            projected = psum.tile([P, R], F32, bufs=1)
            feats_ps[i] = projected
            for b in range(2):
                nc.tensor.matmul_mx(
                    out=projected[:],
                    lhsT=hf_codes[i][:, b].bitcast(F8X4),
                    lhsT_scale=hf_scales[i][:, b],
                    rhs=proj_w[:, b].bitcast(F4X4),
                    rhs_scale=proj_s[:, b],
                    start=(b == 0),
                    stop=(b == 1),
                )

        def store_features(i):
            feats = work.tile([P, R], F32, bufs=3, align_bytes=ALIGN)
            nc.scalar.copy(out=feats[:], in_=feats_ps[i][:])
            nc.sync.dma_start(out=out_0.rearrange("(g p t) r -> g t p r", p=P, t=4)[i // 4, i % 4], in_=feats[:])

        def interleave_h(n):
            g, d0 = n // 4, QUARTER * (n % 4)
            ht_i = work.tile([P, QUARTER, 4], BF16, bufs=3, align_bytes=ALIGN)
            ht_inter[n] = ht_i
            on_scalar = n % 3 != 1 and g < GROUPS - 1
            copy = nc.scalar.copy if on_scalar else nc.vector.tensor_copy
            copy(
                out=ht_i[:].rearrange("p (n i) t -> p n t i", i=4),
                in_=h_rows[g][:, :, d0 : d0 + QUARTER].rearrange("p t (n i) -> p n t i", i=4),
            )

        def quantize_tokens(n):
            g, d0 = n // 4, QUARTER * (n % 4)
            nc.vector.quantize_mx(
                out=h_codes[g][:, d0 : d0 + QUARTER].bitcast(F8X4),
                scales=h_scales[g][:, d0 : d0 + QUARTER],
                in_=ht_inter[n][:].rearrange("p d t -> p (d t)"),
            )

        def pool_pass(g, h):
            for a in range(2):
                nc.tensor.matmul_mx(
                    out=latents_ps[a, h][:],
                    lhsT=p_codes[:, g, a * P : (a + 1) * P].bitcast(F8X4),
                    lhsT_scale=p_scales[:, g, a * P : (a + 1) * P],
                    rhs=h_codes[g][:, h * HALF : (h + 1) * HALF].bitcast(F8X4),
                    rhs_scale=h_scales[g][:, h * HALF : (h + 1) * HALF],
                    start=(g == 0),
                    stop=(g == GROUPS - 1),
                )

        def store_latents(a, h):
            lat = work.tile([P, HALF], F32, bufs=4, align_bytes=ALIGN)
            copy = nc.vector.tensor_copy if a == 0 else nc.scalar.copy
            copy(
                out=lat[:].rearrange("p (q u e) -> p q u e", u=2, e=2),
                in_=latents_ps[a, h][:].rearrange("p (u q e) -> p q u e", u=2, e=2),
            )
            nc.sync.dma_start(out=out_1[a * P : (a + 1) * P, h * HALF : (h + 1) * HALF], in_=lat[:])

        scalar, vector = nc.scalar.copy, nc.vector.tensor_copy
        interleave_w(1, 0, vector)
        interleave_w(2, 1, scalar)
        quantize_w(1, 0)
        interleave_w(2, 0, scalar)
        interleave_w(1, 1, vector)
        quantize_w(1, 1)
        turn_pool(0)
        quantize_w(2, 1)
        empty_pool(0)
        quantize_w(2, 0)
        turn_pool(1)
        interleave_w(0, 1, vector)
        quantize_pool(0)
        nc.vector.tensor_copy(out=gain_col[:], in_=gain_raw[:].rearrange("p g t -> p (g t)"))
        empty_pool(1)
        interleave_w(0, 0, vector)
        turn_pool(2)
        turn_pool(3)
        empty_pool(2)
        quantize_pool(1)
        quantize_w(0, 1)
        quantize_w(0, 0)
        widen_x(0)
        empty_pool(3)

        steps = (
            (turn_x, 1, (0,)),
            (widen_x, 2, ()),
            (store_features, -3, ()),
            (empty_x, 1, (0,)),
            (turn_x, 1, (1,)),
            (turn_h, -1, ()),
            (place, 1, (0,)),
            (embed, 0, (0,)),
            (scale_term, 1, (0,)),
            (embed, 0, (1,)),
            (empty_x, 1, (1,)),
            (interleave_h, -4, ()),
            (quantize_features, -2, ()),
            (place, 1, (1,)),
            (scale_term, 1, (1,)),
            (quantize_tokens, -5, ()),
            (empty_h, -1, ()),
            (finish_h, 0, (0,)),
            (project, -2, ()),
            (finish_h, 0, (1,)),
            (quantize_x, 1, (0,)),
            (quantize_x, 1, (1,)),
        )
        for i in range(-1, TILES + 5):
            if i in (2, 3):
                quantize_pool(i)
            if i == TILES:
                banks = (("x_turned", 2), ("x_turned", 2), ("placed", 1), ("acc", 2))
                for n, (tag, bufs) in enumerate(banks):
                    bank = psum.tile([P, HALF], F32, tag=tag, bufs=bufs)
                    latents_ps[n // 2, n % 2] = bank
            if TILES <= i < TILES + 3:
                for h in range(2):
                    pool_pass(i - TILES, h)
            for stage, ahead, part in steps:
                if 0 <= i + ahead < TILES:
                    stage(i + ahead, *part)
            if i == TILES + 2:
                pool_pass(3, 0)
        pool_pass(3, 1)
        for h in range(2):
            for a in range(2):
                store_latents(a, h)
